import numpy as np
import ml_dtypes


def mxq(x, axis, fmt="e4m3"):
    dtype, down = {"e4m3": (ml_dtypes.float8_e4m3fn, 7), "e5m2": (ml_dtypes.float8_e5m2, 14)}[fmt]
    v = np.moveaxis(np.asarray(x, np.float32).astype(ml_dtypes.bfloat16).astype(np.float64), axis, -1)
    blocks = v.reshape(v.shape[:-1] + (-1, 32))
    amax = np.abs(blocks).max(-1, keepdims=True)
    byte = np.maximum(np.where(amax > 0, np.frexp(amax)[1] - 1 + 127, 0) - down, 1)
    scale = np.exp2(byte - 127.0)
    codes = (blocks / scale).astype(np.float32).astype(dtype).astype(np.float64)
    return np.moveaxis((codes * scale).reshape(v.shape), -1, axis)


WIDE = False


def mx_kscale(k):
    if not WIDE:
        return np.ones(k)
    levels = np.array([30, -30])
    if k % 512:
        return np.exp2(np.random.permutation(np.resize(levels, k // 32))).repeat(32)
    a = np.empty((k // 512, 16))
    for p in range(k // 512):
        a[p, :8] = np.random.permutation(np.resize(levels, 8))
        for g in range(8):
            far = levels[np.abs(levels - a[p, g]) >= 10]
            a[p, g + 8] = far[np.random.randint(len(far))]
    return np.exp2(a.ravel()).repeat(32)


def f64(x):
    return np.asarray(x).astype(np.float64)


def striped(idx):
    return np.tile(idx.reshape(-1, 16).T, (8, 1)).astype(np.uint16)


def unstriped(offs):
    return offs[:16].T.reshape(-1).astype(np.int64)


def bf(x):
    return np.asarray(x, np.float32).astype(ml_dtypes.bfloat16)


E2M1 = np.array([0.0, 0.5, 1.0, 1.5, 2.0, 3.0, 4.0, 6.0, -0.0, -0.5, -1.0, -1.5, -2.0, -3.0, -4.0, -6.0])


def pack_weight(w, fmt):
    k, n = w.shape
    w = f64(bf(w)).reshape(k // 32, 32, n)
    amax = np.abs(w).max(1)
    if fmt in ("e4m3", "e5m2"):
        byte = np.frexp(amax)[1] - 1 + 127 - (7 if fmt == "e4m3" else 14)
    else:
        mant, ex = np.frexp(amax / 6.0)
        byte = np.where(mant > 0.5, ex, ex - 1) + 127
    byte = np.clip(np.where(amax > 0, byte, 1), 1, 254)
    scaled = (w * np.exp2(127.0 - byte)[:, None, :]).reshape(k, n).astype(np.float32)
    by_word = np.ascontiguousarray(scaled.reshape(k // 512, 128, 4, n).transpose(0, 1, 3, 2))
    if fmt in ("e4m3", "e5m2"):
        words = by_word.astype(ml_dtypes.float8_e4m3fn if fmt == "e4m3" else ml_dtypes.float8_e5m2).view(np.uint8)
    else:
        c = by_word.astype(ml_dtypes.float4_e2m1fn).view(np.uint8) & 0xF
        words = c[..., 0::2] | (c[..., 1::2] << 4)
    return np.ascontiguousarray(words), np.ascontiguousarray(byte.astype(np.uint8).reshape(k // 512, 16, n))


def unpack_weight(words, scales, fmt):
    g, p, n, _ = words.shape
    if fmt in ("e4m3", "e5m2"):
        vals = np.ascontiguousarray(words).view(ml_dtypes.float8_e4m3fn if fmt == "e4m3" else ml_dtypes.float8_e5m2).astype(np.float64)
    else:
        nib = np.empty((g, p, n, 4), np.uint8)
        nib[..., 0::2] = words & 0xF
        nib[..., 1::2] = words >> 4
        vals = E2M1[nib]
    vals = vals * np.repeat(np.exp2(scales.astype(np.float64) - 127.0), 8, axis=1)[..., None]
    return vals.transpose(0, 1, 3, 2).reshape(g * 512, n)


K, T, S, H, N = 1024, 2048, 1024, 1024, 512

def setup_inputs():
    n = np.random.standard_normal
    s = mx_kscale(K)[:, None]
    u = mx_kscale(H)[:, None]
    tab_words, tab_scales = pack_weight(n((K, T)) * np.exp(1.0 * n((1, T))) * s, "e5m2")
    wd_words, wd_scales = pack_weight(0.5 * n((K, N)) / np.sqrt(K) / s, "e4m3")
    return {
        "tab_words": tab_words, "tab_scales": tab_scales,
        "offs": striped(np.random.permutation(T)[:S]),
        "w1": (n((K, H)) / np.sqrt(K) / s).astype(np.float32),
        "b1": (0.3 * n(H)).astype(np.float32),
        "g": (np.random.uniform(0.5, 1.5, H) * u[:, 0]).astype(np.float32),
        "w2": (1.5 * n((H, N)) / np.sqrt(H) / u).astype(np.float32),
        "wd_words": wd_words, "wd_scales": wd_scales,
        "lr": np.exp(0.3 * n(N)).astype(np.float32),
    }

def reference(tab_words, tab_scales, offs, w1, b1, g, w2, wd_words, wd_scales, lr):
    v = unpack_weight(tab_words, tab_scales, "e5m2")[:, unstriped(offs)]
    w1q = mxq(f64(w1), 0, "e4m3")
    w2q = mxq(f64(w2), 0, "e4m3")
    wd = unpack_weight(wd_words, wd_scales, "e4m3")
    a = w1q.T @ v
    h = np.tanh(a + f64(b1)[:, None]) * f64(g)[:, None]
    hq = mxq(h, 0, "e4m3")
    y = w2q.T @ hq + wd.T @ v
    return f64(lr)[:, None] * y

@@ -1,0 +1,277 @@
+from contextlib import ExitStack
+
+import concourse.mybir as mybir
+
+K, T, S, H, N = 1024, 2048, 1024, 1024, 512
+FLOPS = 2 * S * (K * H + H * N + K * N)
+
+F32 = mybir.dt.float32
+BF16 = mybir.dt.bfloat16
+I32 = mybir.dt.int32
+U32 = mybir.dt.uint32
+U16 = mybir.dt.uint16
+U8 = mybir.dt.uint8
+E4M3 = mybir.dt.float8_e4m3fn_x4
+E5M2 = mybir.dt.float8_e5m2_x4
+TANH = mybir.ActivationFunctionType.Tanh
+COPY = mybir.ActivationFunctionType.Copy
+MULT = mybir.AluOpType.mult
+ADD = mybir.AluOpType.add
+
+P = 128
+PACK = 4
+PASS = P * PACK
+COLS = 512
+QUADS = 4
+
+
+def tile_list_meta_adapted_steps_kernel(tc, tab_words, tab_scales, offs, w1, b1, g, w2, wd_words, wd_scales, lr, out):
+    nc = tc.nc
+    with ExitStack() as ctx:
+        keep = ctx.enter_context(tc.tile_pool(name="keep", bufs=1))
+        ring = ctx.enter_context(tc.tile_pool(name="ring", bufs=4))
+        psum = ctx.enter_context(tc.psum_pool(name="psum", bufs=1))
+
+        def sb(shape, dtype, name):
+            return keep.tile(shape, dtype, name=name, align_bytes=64)
+
+        offsets = keep.tile([P, S // 16], U16, name="offsets")
+        nc.sync.dma_start(offsets[:], offs)
+
+        tab_sc = sb([P, T // 4], I32, "tab_sc")
+        moved = sb([P, S // 4], I32, "moved")
+        nc.vector.memset(tab_sc[:], 0)
+        warm = sb([P, 2], F32, "warm")
+        nc.vector.memset(warm[:, 0:1], 0.0)
+        nc.vector.memset(moved[:], 0)
+        nc.scalar.activation(out=warm[:, 1:2], in_=warm[:, 0:1], func=TANH)
+
+        b1_sb = sb([P, 2, PACK], F32, "b1_sb")
+        g_sb = sb([P, 2, PACK], F32, "g_sb")
+
+        def load_vec(dst, src):
+            nc.scalar.dma_start(out=dst[:], in_=src.rearrange("(b p t) -> p b t", b=2, t=PACK))
+
+        def load_lr():
+            with nc.allow_non_contiguous_dma(reason="one rate for each partition"):
+                nc.sync.dma_start(out=lr_sb[:], in_=lr.rearrange("(c p) -> p c", p=P))
+
+        def load_scale_rows(dst, src):
+            for q in range(QUADS):
+                nc.sync.dma_start(out=dst[32 * q : 32 * q + 4, :, :],
+                                  in_=src[:, 4 * q : 4 * q + 4, :].bitcast(I32).rearrange("a r c -> r a c"))
+
+        tab = [sb([P, T], I32, "tab%d" % a) for a in range(2)]
+        def landing(shape, dtype, name):
+            return ring.tile(shape, dtype, name=name, tag="landing", align_bytes=64)
+
+        w1_raw = {(a, b): landing([P, PACK, COLS], F32, "w1_raw%d%d" % (a, b)) for b in range(2) for a in range(2)}
+        wd_all = landing([P, 2, N + N // 4], I32, "wd_all")
+        wd, wd_sc = wd_all[:, :, 0:N], wd_all[:, :, N : N + N // 4]
+        w2_raw = [landing([P, PACK, N], F32, "w2_raw%d" % b) for b in range(2)]
+        lr_sb = landing([P, N // P], F32, "lr_sb")
+
+        def load_tab(a):
+            nc.sync.dma_start(out=tab[a][:], in_=tab_words[a].rearrange("p c i -> p (c i)").bitcast(I32))
+
+        def load_w1(a, b, c0, c1):
+            rows = w1[a * PASS : (a + 1) * PASS, b * COLS + c0 : b * COLS + c1]
+            nc.sync.dma_start(out=w1_raw[a, b][:, :, c0:c1], in_=rows.rearrange("(p j) c -> p j c", j=PACK))
+
+        def load_w2(b, c0, c1):
+            rows = w2[b * PASS : (b + 1) * PASS, c0:c1]
+            nc.sync.dma_start(out=w2_raw[b][:, :, c0:c1], in_=rows.rearrange("(p j) c -> p j c", j=PACK))
+
+        def load_tab_scales():
+            for q in range(QUADS):
+                nc.sync.dma_start(out=tab_sc[32 * q : 32 * q + 8, :], in_=tab_scales[:, 4 * q : 4 * q + 4, :].bitcast(I32))
+
+        def load_wd():
+            nc.vector.memset(wd_sc, 0)
+            nc.sync.dma_start(out=wd, in_=wd_words.rearrange("a p c i -> p a (c i)").bitcast(I32))
+            load_scale_rows(wd_sc, wd_scales)
+
+        load_tab_scales()
+        load_vec(b1_sb, b1)
+        load_vec(g_sb, g)
+        load_tab(0)
+        load_tab(1)
+        load_w1(0, 0, 0, 512)
+        load_w1(1, 0, 0, 256)
+        load_w1(1, 0, 256, 512)
+        load_w1(0, 1, 0, 512)
+        load_w1(1, 1, 0, 512)
+
+        v_codes, v_scales = {}, {}
+
+        def lists(s):
+            return offsets[:, s * (COLS // 16) : (s + 1) * (COLS // 16)]
+
+        def gather_scales():
+            picked = sb([P, S // 4], I32, "picked")
+            nc.vector.tensor_copy(picked[:].bitcast(U8), tab_sc[:].bitcast(U8).indirect(offsets[:]))
+            for q in range(QUADS):
+                nc.scalar.dma_start(out=moved[32 * q : 32 * q + 4, :], in_=picked[32 * q + 4 : 32 * q + 8, :])
+            for s in range(2):
+                v_scales[0, s] = picked[:].bitcast(U8)[:, s * COLS : (s + 1) * COLS]
+                v_scales[1, s] = moved[:].bitcast(U8)[:, s * COLS : (s + 1) * COLS]
+
+        def gather_words(a, s):
+            v_codes[a, s] = sb([P, COLS], U32, "v_codes%d%d" % (a, s))
+            nc.vector.tensor_copy(v_codes[a, s][:], tab[a][:].bitcast(U32).indirect(lists(s)))
+
+        def cast(engine, dst, src):
+            if engine == "scalar":
+                nc.scalar.copy(out=dst, in_=src)
+            else:
+                nc.vector.tensor_copy(out=dst, in_=src)
+
+        rounded, codes, scales = {}, {}, {}
+
+        def staged(key):
+            if key not in rounded:
+                rounded[key] = sb([P, PACK * COLS], BF16, "rounded_" + key)
+            return rounded[key]
+
+        def round_w1(engine, a, b, m0, m1):
+            dst = staged("w1_%d%d" % (a, b))[:].rearrange("p (t m j) -> p m j t", t=PACK, j=PACK)[:, m0:m1, :, :]
+            src = w1_raw[a, b][:].rearrange("p j (m t) -> p m j t", t=PACK)[:, m0:m1, :, :]
+            cast(engine, dst, src)
+
+        def round_w2(engine, b, c0, c1):
+            dst = staged("w2_%d" % b)[:].rearrange("p (c e j) -> p c j e", e=2, j=PACK)[:, c0 // 2 : c1 // 2, :, :]
+            src = w2_raw[b][:].rearrange("p j (c e) -> p c j e", e=2)[:, c0 // 2 : c1 // 2, :, :]
+            cast(engine, dst, src)
+
+        def quantize(key, c0=0, c1=COLS):
+            if key not in codes:
+                codes[key] = sb([P, COLS], U32, "codes_" + key)
+                scales[key] = sb([P, COLS], U8, "scales_" + key)
+            nc.vector.quantize_mx(out=codes[key][:, c0:c1].bitcast(E4M3), scales=scales[key][:, c0:c1],
+                                  in_=rounded[key][:, PACK * c0 : PACK * c1])
+
+        banks = {}
+
+        def bank(i):
+            banks[i] = psum.tile([P, COLS], F32, name="bank%d" % i, tag="bank%d" % i)
+            return banks[i]
+
+        def hidden_pass(b, s, t, a, bk):
+            acc = bank(bk) if a == 0 else banks[bk]
+            key = "w1_%d%d" % (a, b)
+            cols = slice(t * P, (t + 1) * P)
+            nc.tensor.matmul_mx(out=acc[:], lhsT=codes[key][:, cols].bitcast(E4M3), lhsT_scale=scales[key][:, cols],
+                                rhs=v_codes[a, s][:].bitcast(E5M2), rhs_scale=v_scales[a, s],
+                                start=(a == 0), stop=(a == 1))
+
+        tanh_out, gained = {}, {}
+
+        def tanh_tile(b, s, t, bk):
+            if (b, s) not in tanh_out:
+                tanh_out[b, s] = sb([P, PACK, COLS], F32, "tanh_out%d%d" % (b, s))
+            nc.scalar.activation(out=tanh_out[b, s][:, t, :], in_=banks[bk][:], func=TANH, bias=b1_sb[:, b, t : t + 1])
+
+        def gain(b, s, c0, c1):
+            dst = staged("h_%d%d" % (b, s))[:].rearrange("p (c e t) -> p c t e", e=2, t=PACK)[:, c0 // 2 : c1 // 2, :, :]
+            src = tanh_out[b, s][:].rearrange("p t (c e) -> p c t e", e=2)[:, c0 // 2 : c1 // 2, :, :]
+            gains = g_sb[:, b, :].unsqueeze(1).unsqueeze(3).to_broadcast([P, (c1 - c0) // 2, PACK, 2])
+            nc.vector.tensor_tensor(out=dst, in0=src, in1=gains, op=MULT)
+
+        def gain_plane(b, s, t, c0, c1):
+            if (b, s) not in gained:
+                gained[b, s] = sb([P, PACK, COLS], BF16, "gained%d%d" % (b, s))
+            nc.scalar.activation(out=gained[b, s][:, t, c0:c1], in_=tanh_out[b, s][:, t, c0:c1], func=COPY,
+                                 scale=g_sb[:, b, t : t + 1])
+
+        def interleave(b, s, c0, c1):
+            dst = staged("h_%d%d" % (b, s))[:].rearrange("p (c e t) -> p c t e", e=4, t=PACK)[:, c0 // 4 : c1 // 4, :, :]
+            src = gained[b, s][:].rearrange("p t (c e) -> p c t e", e=4)[:, c0 // 4 : c1 // 4, :, :]
+            nc.vector.tensor_copy(out=dst, in_=src)
+
+        def direct_pass(s, n, a, bk):
+            acc = bank(bk) if a == 0 else banks[bk]
+            cols = slice(n * P, (n + 1) * P)
+            nc.tensor.matmul_mx(out=acc[:], lhsT=wd[:, a, cols].bitcast(E4M3),
+                                lhsT_scale=wd_sc[:, a, :].bitcast(U8)[:, cols],
+                                rhs=v_codes[a, s][:].bitcast(E5M2), rhs_scale=v_scales[a, s],
+                                start=(a == 0), stop=False)
+
+        def branch_pass(b, s, n, bk, c0, c1):
+            cols = slice(n * P, (n + 1) * P)
+            wk, hk = "w2_%d" % b, "h_%d%d" % (b, s)
+            nc.tensor.matmul_mx(out=banks[bk][:, c0:c1], lhsT=codes[wk][:, cols].bitcast(E4M3), lhsT_scale=scales[wk][:, cols],
+                                rhs=codes[hk][:, c0:c1].bitcast(E4M3), rhs_scale=scales[hk][:, c0:c1],
+                                start=False, stop=(b == 1))
+
+        def finish(engine, s, n, bk, c0, c1):
+            res = sb([P, c1 - c0], F32, "res%d%d_%d" % (s, n, c0))
+            if engine == "scalar":
+                nc.scalar.activation(out=res[:], in_=banks[bk][:, c0:c1], func=COPY, scale=lr_sb[:, n : n + 1])
+            else:
+                nc.vector.tensor_scalar(out=res[:], in0=banks[bk][:, c0:c1], scalar1=lr_sb[:, n : n + 1], scalar2=None, op0=MULT)
+            nc.sync.dma_start(out=out[n * P : (n + 1) * P, s * COLS + c0 : s * COLS + c1], in_=res[:])
+
+        gather_scales()
+        for a in range(2):
+            for s in range(2):
+                gather_words(a, s)
+        round_w1("scalar", 0, 0, 0, 128)
+        quantize("w1_00")
+        round_w1("scalar", 1, 0, 0, 64)
+        round_w1("vector", 1, 0, 64, 128)
+        quantize("w1_10")
+        load_wd()
+        load_w2(0, 0, 512)
+        for a in range(2):
+            for t in range(PACK):
+                hidden_pass(0, 0, t, a, t)
+        for t in range(PACK):
+            tanh_tile(0, 0, t, t)
+        for t in range(PACK):
+            hidden_pass(0, 1, t, 0, 4 + t)
+            hidden_pass(0, 1, t, 1, 4 + t)
+            tanh_tile(0, 1, t, 4 + t)
+        round_w1("vector", 0, 1, 0, 128)
+        load_w2(1, 0, 512)
+        quantize("w1_01")
+        round_w1("vector", 1, 1, 0, 128)
+        load_lr()
+        gain(0, 0, 0, 512)
+        quantize("w1_11")
+        round_w2("scalar", 0, 0, 512)
+        gain(0, 1, 0, 512)
+        for a in range(2):
+            for t in range(PACK):
+                hidden_pass(1, 0, t, a, t)
+        for t in range(PACK):
+            tanh_tile(1, 0, t, t)
+        for n in range(4):
+            direct_pass(0, n, 0, 4 + n)
+            direct_pass(0, n, 1, 4 + n)
+        quantize("h_00")
+        quantize("w2_0")
+        quantize("h_01")
+        round_w2("vector", 1, 0, 256)
+        gain(1, 0, 0, 512)
+        for t in range(PACK):
+            hidden_pass(1, 1, t, 0, t)
+            hidden_pass(1, 1, t, 1, t)
+            tanh_tile(1, 1, t, t)
+            gain_plane(1, 1, t, 0, 512)
+        for n in range(4):
+            branch_pass(0, 0, n, 4 + n, 0, 512)
+        round_w2("vector", 1, 256, 512)
+        quantize("h_10")
+        quantize("w2_1")
+        for n in range(4):
+            direct_pass(1, n, 0, n)
+            direct_pass(1, n, 1, n)
+            branch_pass(0, 1, n, n, 0, 512)
+        for n in range(4):
+            branch_pass(1, 0, n, 4 + n, 0, 512)
+            finish("scalar", 0, n, 4 + n, 0, 512)
+        interleave(1, 1, 0, 512)
+        quantize("h_11")
+        for n in range(4):
+            branch_pass(1, 1, n, n, 0, 512)
+            finish("vector" if n % 2 else "scalar", 1, n, n, 0, 512)

@@ -1,6 +1,7 @@
 from contextlib import ExitStack
 
 import concourse.mybir as mybir
+from concourse.masks import make_identity
 
 K, T, S, H, N = 1024, 2048, 1024, 1024, 512
 FLOPS = 2 * S * (K * H + H * N + K * N)
@@ -29,47 +30,53 @@ def tile_list_meta_adapted_steps_kernel(tc, tab_words, tab_scales, offs, w1, b1,
     nc = tc.nc
     with ExitStack() as ctx:
         keep = ctx.enter_context(tc.tile_pool(name="keep", bufs=1))
-        ring = ctx.enter_context(tc.tile_pool(name="ring", bufs=4))
         psum = ctx.enter_context(tc.psum_pool(name="psum", bufs=1))
 
+        shared = {"w1_raw11": "slot_a", "rounded_h_00": "slot_a", "w2_raw0": "slot_b", "tanh_out10": "slot_b",
+                  "rounded_w1_11": "slot_c", "rounded_h_01": "slot_c", "rounded_w2_0": "slot_e", "rounded_h_10": "slot_e"}
+
         def sb(shape, dtype, name):
-            return keep.tile(shape, dtype, name=name, align_bytes=64)
+            return keep.tile(shape, dtype, name=name, tag=shared.get(name, name), align_bytes=64)
 
         offsets = keep.tile([P, S // 16], U16, name="offsets")
         nc.sync.dma_start(offsets[:], offs)
 
         tab_sc = sb([P, T // 4], I32, "tab_sc")
         moved = sb([P, S // 4], I32, "moved")
+        wd_sc = sb([P, 2, N // 4], I32, "wd_sc")
         nc.vector.memset(tab_sc[:], 0)
-        warm = sb([P, 2], F32, "warm")
-        nc.vector.memset(warm[:, 0:1], 0.0)
+        nc.vector.memset(wd_sc[:], 0)
         nc.vector.memset(moved[:], 0)
-        nc.scalar.activation(out=warm[:, 1:2], in_=warm[:, 0:1], func=TANH)
+        rows = sb([P, COLS + P], F32, "rows")
+        nc.vector.memset(rows[:], 0.0)
+        ident = sb([P, P], F32, "ident")
+        make_identity(nc, ident[:])
+        per_r = sb([P, 4, PACK], F32, "per_r")
+        lr_sb = sb([P, N // P], F32, "lr_sb")
 
-        b1_sb = sb([P, 2, PACK], F32, "b1_sb")
-        g_sb = sb([P, 2, PACK], F32, "g_sb")
+        def load_vectors():
+            nc.gpsimd.dma_start(out=rows[0:2, 0:COLS], in_=b1.rearrange("(b c) -> b c", b=2))
+            nc.gpsimd.dma_start(out=rows[2:4, 0:COLS], in_=g.rearrange("(b c) -> b c", b=2))
+            nc.gpsimd.dma_start(out=rows[0:4, COLS : COLS + P], in_=lr.rearrange("(n p) -> n p", p=P))
 
-        def load_vec(dst, src):
-            nc.scalar.dma_start(out=dst[:], in_=src.rearrange("(b p t) -> p b t", b=2, t=PACK))
-
-        def load_lr():
-            with nc.allow_non_contiguous_dma(reason="one rate for each partition"):
-                nc.sync.dma_start(out=lr_sb[:], in_=lr.rearrange("(c p) -> p c", p=P))
+        def turn_vectors():
+            turned = psum.tile([P, PACK, P], F32, name="turned", tag="bank0")
+            turned_lr = psum.tile([P, P], F32, name="turned_lr", tag="bank1")
+            for t in range(PACK):
+                nc.tensor.transpose(turned[:, t, :], rows[:, t:COLS:PACK], ident[:])
+            nc.tensor.transpose(turned_lr[:], rows[:, COLS : COLS + P], ident[:])
+            nc.scalar.activation(out=per_r[:], in_=turned[:, :, 0:4].rearrange("p t k -> p k t"), func=COPY)
+            nc.scalar.activation(out=lr_sb[:], in_=turned_lr[:, 0:4], func=COPY)
 
         def load_scale_rows(dst, src):
             for q in range(QUADS):
-                nc.sync.dma_start(out=dst[32 * q : 32 * q + 4, :, :],
+                nc.gpsimd.dma_start(out=dst[32 * q : 32 * q + 4, :, :],
                                   in_=src[:, 4 * q : 4 * q + 4, :].bitcast(I32).rearrange("a r c -> r a c"))
 
         tab = [sb([P, T], I32, "tab%d" % a) for a in range(2)]
-        def landing(shape, dtype, name):
-            return ring.tile(shape, dtype, name=name, tag="landing", align_bytes=64)
-
-        w1_raw = {(a, b): landing([P, PACK, COLS], F32, "w1_raw%d%d" % (a, b)) for b in range(2) for a in range(2)}
-        wd_all = landing([P, 2, N + N // 4], I32, "wd_all")
-        wd, wd_sc = wd_all[:, :, 0:N], wd_all[:, :, N : N + N // 4]
-        w2_raw = [landing([P, PACK, N], F32, "w2_raw%d" % b) for b in range(2)]
-        lr_sb = landing([P, N // P], F32, "lr_sb")
+        w1_raw = {(a, b): sb([P, PACK, COLS], F32, "w1_raw%d%d" % (a, b)) for a in range(2) for b in range(2)}
+        w2_raw = [sb([P, PACK, N], F32, "w2_raw%d" % b) for b in range(2)]
+        wd = sb([P, 2, N], I32, "wd")
 
         def load_tab(a):
             nc.sync.dma_start(out=tab[a][:], in_=tab_words[a].rearrange("p c i -> p (c i)").bitcast(I32))
@@ -83,24 +90,25 @@ def tile_list_meta_adapted_steps_kernel(tc, tab_words, tab_scales, offs, w1, b1,
             nc.sync.dma_start(out=w2_raw[b][:, :, c0:c1], in_=rows.rearrange("(p j) c -> p j c", j=PACK))
 
         def load_tab_scales():
-            for q in range(QUADS):
-                nc.sync.dma_start(out=tab_sc[32 * q : 32 * q + 8, :], in_=tab_scales[:, 4 * q : 4 * q + 4, :].bitcast(I32))
+            by_row = tab_scales.bitcast(I32).rearrange("a (q r) c -> r q a c", r=4)
+            for r in range(4):
+                nc.sync.dma_start(out=tab_sc[r:P:16, :], in_=by_row[r])
 
         def load_wd():
-            nc.vector.memset(wd_sc, 0)
-            nc.sync.dma_start(out=wd, in_=wd_words.rearrange("a p c i -> p a (c i)").bitcast(I32))
-            load_scale_rows(wd_sc, wd_scales)
+            nc.sync.dma_start(out=wd[:], in_=wd_words.rearrange("a p c i -> p a (c i)").bitcast(I32))
 
         load_tab_scales()
-        load_vec(b1_sb, b1)
-        load_vec(g_sb, g)
-        load_tab(0)
-        load_tab(1)
+        load_vectors()
+        load_scale_rows(wd_sc, wd_scales)
         load_w1(0, 0, 0, 512)
-        load_w1(1, 0, 0, 256)
-        load_w1(1, 0, 256, 512)
+        load_tab(0)
+        load_w1(1, 0, 0, 512)
+        load_tab(1)
         load_w1(0, 1, 0, 512)
         load_w1(1, 1, 0, 512)
+        load_w2(0, 0, 512)
+        load_wd()
+        load_w2(1, 0, 512)
 
         v_codes, v_scales = {}, {}
 
@@ -111,7 +119,7 @@ def tile_list_meta_adapted_steps_kernel(tc, tab_words, tab_scales, offs, w1, b1,
             picked = sb([P, S // 4], I32, "picked")
             nc.vector.tensor_copy(picked[:].bitcast(U8), tab_sc[:].bitcast(U8).indirect(offsets[:]))
             for q in range(QUADS):
-                nc.scalar.dma_start(out=moved[32 * q : 32 * q + 4, :], in_=picked[32 * q + 4 : 32 * q + 8, :])
+                nc.scalar.dma_start(out=moved[32 * q : 32 * q + 4, :], in_=picked[32 * q + 16 : 32 * q + 20, :])
             for s in range(2):
                 v_scales[0, s] = picked[:].bitcast(U8)[:, s * COLS : (s + 1) * COLS]
                 v_scales[1, s] = moved[:].bitcast(U8)[:, s * COLS : (s + 1) * COLS]
@@ -122,7 +130,7 @@ def tile_list_meta_adapted_steps_kernel(tc, tab_words, tab_scales, offs, w1, b1,
 
         def cast(engine, dst, src):
             if engine == "scalar":
-                nc.scalar.copy(out=dst, in_=src)
+                nc.scalar.activation(out=dst, in_=src, func=COPY)
             else:
                 nc.vector.tensor_copy(out=dst, in_=src)
 
@@ -169,19 +177,19 @@ def tile_list_meta_adapted_steps_kernel(tc, tab_words, tab_scales, offs, w1, b1,
         def tanh_tile(b, s, t, bk):
             if (b, s) not in tanh_out:
                 tanh_out[b, s] = sb([P, PACK, COLS], F32, "tanh_out%d%d" % (b, s))
-            nc.scalar.activation(out=tanh_out[b, s][:, t, :], in_=banks[bk][:], func=TANH, bias=b1_sb[:, b, t : t + 1])
+            nc.scalar.activation(out=tanh_out[b, s][:, t, :], in_=banks[bk][:], func=TANH, bias=per_r[:, b, t : t + 1])
 
         def gain(b, s, c0, c1):
             dst = staged("h_%d%d" % (b, s))[:].rearrange("p (c e t) -> p c t e", e=2, t=PACK)[:, c0 // 2 : c1 // 2, :, :]
             src = tanh_out[b, s][:].rearrange("p t (c e) -> p c t e", e=2)[:, c0 // 2 : c1 // 2, :, :]
-            gains = g_sb[:, b, :].unsqueeze(1).unsqueeze(3).to_broadcast([P, (c1 - c0) // 2, PACK, 2])
+            gains = per_r[:, 2 + b, :].unsqueeze(1).unsqueeze(3).to_broadcast([P, (c1 - c0) // 2, PACK, 2])
             nc.vector.tensor_tensor(out=dst, in0=src, in1=gains, op=MULT)
 
         def gain_plane(b, s, t, c0, c1):
             if (b, s) not in gained:
                 gained[b, s] = sb([P, PACK, COLS], BF16, "gained%d%d" % (b, s))
             nc.scalar.activation(out=gained[b, s][:, t, c0:c1], in_=tanh_out[b, s][:, t, c0:c1], func=COPY,
-                                 scale=g_sb[:, b, t : t + 1])
+                                 scale=per_r[:, 2 + b, t : t + 1])
 
         def interleave(b, s, c0, c1):
             dst = staged("h_%d%d" % (b, s))[:].rearrange("p (c e t) -> p c t e", e=4, t=PACK)[:, c0 // 4 : c1 // 4, :, :]
@@ -201,7 +209,7 @@ def tile_list_meta_adapted_steps_kernel(tc, tab_words, tab_scales, offs, w1, b1,
             wk, hk = "w2_%d" % b, "h_%d%d" % (b, s)
             nc.tensor.matmul_mx(out=banks[bk][:, c0:c1], lhsT=codes[wk][:, cols].bitcast(E4M3), lhsT_scale=scales[wk][:, cols],
                                 rhs=codes[hk][:, c0:c1].bitcast(E4M3), rhs_scale=scales[hk][:, c0:c1],
-                                start=False, stop=(b == 1))
+                                start=False, stop=(b == 1 and c1 == COLS))
 
         def finish(engine, s, n, bk, c0, c1):
             res = sb([P, c1 - c0], F32, "res%d%d_%d" % (s, n, c0))
@@ -212,66 +220,65 @@ def tile_list_meta_adapted_steps_kernel(tc, tab_words, tab_scales, offs, w1, b1,
             nc.sync.dma_start(out=out[n * P : (n + 1) * P, s * COLS + c0 : s * COLS + c1], in_=res[:])
 
         gather_scales()
-        for a in range(2):
-            for s in range(2):
-                gather_words(a, s)
+        gather_words(0, 0)
         round_w1("scalar", 0, 0, 0, 128)
+        turn_vectors()
         quantize("w1_00")
+        gather_words(0, 1)
         round_w1("scalar", 1, 0, 0, 64)
         round_w1("vector", 1, 0, 64, 128)
         quantize("w1_10")
-        load_wd()
-        load_w2(0, 0, 512)
-        for a in range(2):
+        gather_words(1, 0)
+        gather_words(1, 1)
+        for s in range(2):
             for t in range(PACK):
-                hidden_pass(0, 0, t, a, t)
-        for t in range(PACK):
-            tanh_tile(0, 0, t, t)
-        for t in range(PACK):
-            hidden_pass(0, 1, t, 0, 4 + t)
-            hidden_pass(0, 1, t, 1, 4 + t)
-            tanh_tile(0, 1, t, 4 + t)
+                hidden_pass(0, s, t, 0, 4 * s + t)
+        for s in range(2):
+            for t in range(PACK):
+                hidden_pass(0, s, t, 1, 4 * s + t)
+                tanh_tile(0, s, t, 4 * s + t)
         round_w1("vector", 0, 1, 0, 128)
-        load_w2(1, 0, 512)
         quantize("w1_01")
         round_w1("vector", 1, 1, 0, 128)
-        load_lr()
-        gain(0, 0, 0, 512)
         quantize("w1_11")
-        round_w2("scalar", 0, 0, 512)
-        gain(0, 1, 0, 512)
+        round_w2("scalar", 0, 0, 256)
+        round_w2("vector", 0, 256, 512)
+        quantize("w2_0")
         for a in range(2):
             for t in range(PACK):
                 hidden_pass(1, 0, t, a, t)
+        round_w2("scalar", 1, 0, 512)
+        quantize("w2_1")
+        gain(0, 0, 0, 512)
+        quantize("h_00")
         for t in range(PACK):
             tanh_tile(1, 0, t, t)
-        for n in range(4):
-            direct_pass(0, n, 0, 4 + n)
-            direct_pass(0, n, 1, 4 + n)
-        quantize("h_00")
-        quantize("w2_0")
-        quantize("h_01")
-        round_w2("vector", 1, 0, 256)
         gain(1, 0, 0, 512)
+        quantize("h_10")
         for t in range(PACK):
             hidden_pass(1, 1, t, 0, t)
             hidden_pass(1, 1, t, 1, t)
+        for t in range(PACK):
             tanh_tile(1, 1, t, t)
-            gain_plane(1, 1, t, 0, 512)
+            gain_plane(1, 1, t, 256, 512)
+        gain(0, 1, 0, 512)
+        quantize("h_01")
+        gain(1, 1, 0, 256)
+        interleave(1, 1, 256, 512)
+        quantize("h_11")
+        for n in range(4):
+            direct_pass(0, n, 0, 4 + n)
+            direct_pass(0, n, 1, 4 + n)
         for n in range(4):
             branch_pass(0, 0, n, 4 + n, 0, 512)
-        round_w2("vector", 1, 256, 512)
-        quantize("h_10")
-        quantize("w2_1")
-        for n in range(4):
-            direct_pass(1, n, 0, n)
-            direct_pass(1, n, 1, n)
-            branch_pass(0, 1, n, n, 0, 512)
         for n in range(4):
             branch_pass(1, 0, n, 4 + n, 0, 512)
             finish("scalar", 0, n, 4 + n, 0, 512)
-        interleave(1, 1, 0, 512)
-        quantize("h_11")
+        for n in range(4):
+            direct_pass(1, n, 0, n)
+            direct_pass(1, n, 1, n)
+        for n in range(4):
+            branch_pass(0, 1, n, n, 0, 512)
         for n in range(4):
             branch_pass(1, 1, n, n, 0, 512)
             finish("vector" if n % 2 else "scalar", 1, n, n, 0, 512)

@@ -32,8 +32,8 @@ def tile_list_meta_adapted_steps_kernel(tc, tab_words, tab_scales, offs, w1, b1,
         keep = ctx.enter_context(tc.tile_pool(name="keep", bufs=1))
         psum = ctx.enter_context(tc.psum_pool(name="psum", bufs=1))
 
-        shared = {"w1_raw11": "slot_a", "rounded_h_00": "slot_a", "w2_raw0": "slot_b", "tanh_out10": "slot_b",
-                  "rounded_w1_11": "slot_c", "rounded_h_01": "slot_c", "rounded_w2_0": "slot_e", "rounded_h_10": "slot_e"}
+        shared = {"rounded_h_00": "w1_raw11", "rounded_h_10": "w2_raw0", "gained11": "w2_raw1", "gained01": "rounded_w2_0", "rounded_h_01": "tanh_out10", "v_codes11": "rounded_w1_10",
+                  "picked1": "tab0"}
 
         def sb(shape, dtype, name):
             return keep.tile(shape, dtype, name=name, tag=shared.get(name, name), align_bytes=64)
@@ -42,31 +42,28 @@ def tile_list_meta_adapted_steps_kernel(tc, tab_words, tab_scales, offs, w1, b1,
         nc.sync.dma_start(offsets[:], offs)
 
         tab_sc = sb([P, T // 4], I32, "tab_sc")
-        moved = sb([P, S // 4], I32, "moved")
+        moved = [sb([P, COLS // 4], I32, "moved%d" % s) for s in range(2)]
         wd_sc = sb([P, 2, N // 4], I32, "wd_sc")
+        rows = sb([P, COLS], F32, "rows")
         nc.vector.memset(tab_sc[:], 0)
-        nc.vector.memset(wd_sc[:], 0)
-        nc.vector.memset(moved[:], 0)
-        rows = sb([P, COLS + P], F32, "rows")
         nc.vector.memset(rows[:], 0.0)
+        nc.vector.memset(wd_sc[:], 0)
+        for s in range(2):
+            nc.vector.memset(moved[s][96:P, :], 0)
         ident = sb([P, P], F32, "ident")
         make_identity(nc, ident[:])
         per_r = sb([P, 4, PACK], F32, "per_r")
         lr_sb = sb([P, N // P], F32, "lr_sb")
 
         def load_vectors():
-            nc.gpsimd.dma_start(out=rows[0:2, 0:COLS], in_=b1.rearrange("(b c) -> b c", b=2))
-            nc.gpsimd.dma_start(out=rows[2:4, 0:COLS], in_=g.rearrange("(b c) -> b c", b=2))
-            nc.gpsimd.dma_start(out=rows[0:4, COLS : COLS + P], in_=lr.rearrange("(n p) -> n p", p=P))
+            nc.sync.dma_start(out=rows[0:2, 0:COLS], in_=b1.rearrange("(b c) -> b c", b=2))
+            nc.sync.dma_start(out=rows[2:4, 0:COLS], in_=g.rearrange("(b c) -> b c", b=2))
 
         def turn_vectors():
-            turned = psum.tile([P, PACK, P], F32, name="turned", tag="bank0")
-            turned_lr = psum.tile([P, P], F32, name="turned_lr", tag="bank1")
+            turned = psum.tile([P, PACK, P], F32, name="turned", tag="bank7")
             for t in range(PACK):
                 nc.tensor.transpose(turned[:, t, :], rows[:, t:COLS:PACK], ident[:])
-            nc.tensor.transpose(turned_lr[:], rows[:, COLS : COLS + P], ident[:])
             nc.scalar.activation(out=per_r[:], in_=turned[:, :, 0:4].rearrange("p t k -> p k t"), func=COPY)
-            nc.scalar.activation(out=lr_sb[:], in_=turned_lr[:, 0:4], func=COPY)
 
         def load_scale_rows(dst, src):
             for q in range(QUADS):
@@ -97,32 +94,28 @@ def tile_list_meta_adapted_steps_kernel(tc, tab_words, tab_scales, offs, w1, b1,
         def load_wd():
             nc.sync.dma_start(out=wd[:], in_=wd_words.rearrange("a p c i -> p a (c i)").bitcast(I32))
 
+        load_w1(0, 0, 0, 512)
         load_tab_scales()
         load_vectors()
         load_scale_rows(wd_sc, wd_scales)
-        load_w1(0, 0, 0, 512)
         load_tab(0)
-        load_w1(1, 0, 0, 512)
         load_tab(1)
-        load_w1(0, 1, 0, 512)
-        load_w1(1, 1, 0, 512)
-        load_w2(0, 0, 512)
-        load_wd()
-        load_w2(1, 0, 512)
 
         v_codes, v_scales = {}, {}
 
         def lists(s):
             return offsets[:, s * (COLS // 16) : (s + 1) * (COLS // 16)]
 
-        def gather_scales():
-            picked = sb([P, S // 4], I32, "picked")
-            nc.vector.tensor_copy(picked[:].bitcast(U8), tab_sc[:].bitcast(U8).indirect(offsets[:]))
-            for q in range(QUADS):
-                nc.scalar.dma_start(out=moved[32 * q : 32 * q + 4, :], in_=picked[32 * q + 16 : 32 * q + 20, :])
-            for s in range(2):
-                v_scales[0, s] = picked[:].bitcast(U8)[:, s * COLS : (s + 1) * COLS]
-                v_scales[1, s] = moved[:].bitcast(U8)[:, s * COLS : (s + 1) * COLS]
+        picked = {}
+
+        def gather_scales(s):
+            picked[s] = sb([P, COLS // 4], I32, "picked%d" % s)
+            nc.vector.tensor_copy(picked[s][:].bitcast(U8), tab_sc[:].bitcast(U8).indirect(lists(s)))
+            v_scales[0, s] = picked[s][:].bitcast(U8)
+            v_scales[1, s] = moved[s][:].bitcast(U8)
+
+        def move_scales(s):
+            nc.sync.dma_start(out=moved[s][0:112, :], in_=picked[s][16:P, :])
 
         def gather_words(a, s):
             v_codes[a, s] = sb([P, COLS], U32, "v_codes%d%d" % (a, s))
@@ -151,12 +144,12 @@ def tile_list_meta_adapted_steps_kernel(tc, tab_words, tab_scales, offs, w1, b1,
             src = w2_raw[b][:].rearrange("p j (c e) -> p c j e", e=2)[:, c0 // 2 : c1 // 2, :, :]
             cast(engine, dst, src)
 
-        def quantize(key, c0=0, c1=COLS):
+        def quantize(key, c0=0, c1=COLS, part=""):
             if key not in codes:
                 codes[key] = sb([P, COLS], U32, "codes_" + key)
                 scales[key] = sb([P, COLS], U8, "scales_" + key)
             nc.vector.quantize_mx(out=codes[key][:, c0:c1].bitcast(E4M3), scales=scales[key][:, c0:c1],
-                                  in_=rounded[key][:, PACK * c0 : PACK * c1])
+                                  in_=rounded[key + part][:, PACK * c0 : PACK * c1])
 
         banks = {}
 
@@ -179,8 +172,8 @@ def tile_list_meta_adapted_steps_kernel(tc, tab_words, tab_scales, offs, w1, b1,
                 tanh_out[b, s] = sb([P, PACK, COLS], F32, "tanh_out%d%d" % (b, s))
             nc.scalar.activation(out=tanh_out[b, s][:, t, :], in_=banks[bk][:], func=TANH, bias=per_r[:, b, t : t + 1])
 
-        def gain(b, s, c0, c1):
-            dst = staged("h_%d%d" % (b, s))[:].rearrange("p (c e t) -> p c t e", e=2, t=PACK)[:, c0 // 2 : c1 // 2, :, :]
+        def gain(b, s, c0, c1, part=""):
+            dst = staged("h_%d%d" % (b, s) + part)[:].rearrange("p (c e t) -> p c t e", e=2, t=PACK)[:, c0 // 2 : c1 // 2, :, :]
             src = tanh_out[b, s][:].rearrange("p t (c e) -> p c t e", e=2)[:, c0 // 2 : c1 // 2, :, :]
             gains = per_r[:, 2 + b, :].unsqueeze(1).unsqueeze(3).to_broadcast([P, (c1 - c0) // 2, PACK, 2])
             nc.vector.tensor_tensor(out=dst, in0=src, in1=gains, op=MULT)
@@ -219,16 +212,30 @@ def tile_list_meta_adapted_steps_kernel(tc, tab_words, tab_scales, offs, w1, b1,
                 nc.vector.tensor_scalar(out=res[:], in0=banks[bk][:, c0:c1], scalar1=lr_sb[:, n : n + 1], scalar2=None, op0=MULT)
             nc.sync.dma_start(out=out[n * P : (n + 1) * P, s * COLS + c0 : s * COLS + c1], in_=res[:])
 
-        gather_scales()
-        gather_words(0, 0)
-        round_w1("scalar", 0, 0, 0, 128)
+        round_w1("scalar", 0, 0, 40, 128)
+        round_w1("vector", 0, 0, 0, 40)
+        gather_scales(0)
         turn_vectors()
         quantize("w1_00")
+        gather_words(0, 0)
         gather_words(0, 1)
-        round_w1("scalar", 1, 0, 0, 64)
-        round_w1("vector", 1, 0, 64, 128)
-        quantize("w1_10")
+        gather_scales(1)
+        load_w1(1, 0, 0, 512)
+        move_scales(0)
+        load_w1(0, 1, 0, 512)
+        move_scales(1)
+        load_w1(1, 1, 0, 512)
+        load_wd()
+        load_w2(0, 0, 512)
+        load_w2(1, 0, 512)
+        with nc.allow_non_contiguous_dma(reason="one rate for each partition"):
+            nc.sync.dma_start(out=lr_sb[:], in_=lr.rearrange("(n p) -> p n", p=P))
         gather_words(1, 0)
+        round_w1("scalar", 1, 0, 88, 128)
+        round_w1("vector", 1, 0, 0, 88)
+        quantize("w1_10", 0, 128)
+        quantize("w1_10", 128, 256)
+        quantize("w1_10", 256, 512)
         gather_words(1, 1)
         for s in range(2):
             for t in range(PACK):
@@ -240,45 +247,52 @@ def tile_list_meta_adapted_steps_kernel(tc, tab_words, tab_scales, offs, w1, b1,
         round_w1("vector", 0, 1, 0, 128)
         quantize("w1_01")
         round_w1("vector", 1, 1, 0, 128)
-        quantize("w1_11")
-        round_w2("scalar", 0, 0, 256)
-        round_w2("vector", 0, 256, 512)
-        quantize("w2_0")
-        for a in range(2):
+        quantize("w1_11", 0, 256)
+        quantize("w1_11", 256, 512)
+        for s in range(2):
             for t in range(PACK):
-                hidden_pass(1, 0, t, a, t)
-        round_w2("scalar", 1, 0, 512)
-        quantize("w2_1")
+                hidden_pass(1, s, t, 0, 4 * s + t)
+        for s in range(2):
+            for t in range(PACK):
+                hidden_pass(1, s, t, 1, 4 * s + t)
+                tanh_tile(1, s, t, 4 * s + t)
         gain(0, 0, 0, 512)
+        round_w2("vector", 0, 0, 512)
         quantize("h_00")
-        for t in range(PACK):
-            tanh_tile(1, 0, t, t)
+        quantize("w2_0")
         gain(1, 0, 0, 512)
+        round_w2("scalar", 1, 0, 512)
         quantize("h_10")
+        quantize("w2_1")
+        for n in range(4):
+            direct_pass(0, n, 0, n)
+            direct_pass(0, n, 1, n)
+        for n in range(4):
+            branch_pass(0, 0, n, n, 0, 512)
+        for n in range(4):
+            direct_pass(1, n, 0, 4 + n)
+            direct_pass(1, n, 1, 4 + n)
+        for n in range(4):
+            branch_pass(1, 0, n, n, 0, 512)
+        for c0 in (0, 256):
+            for t in range(PACK):
+                gain_plane(1, 1, t, c0, c0 + 256)
         for t in range(PACK):
-            hidden_pass(1, 1, t, 0, t)
-            hidden_pass(1, 1, t, 1, t)
-        for t in range(PACK):
-            tanh_tile(1, 1, t, t)
-            gain_plane(1, 1, t, 256, 512)
-        gain(0, 1, 0, 512)
-        quantize("h_01")
-        gain(1, 1, 0, 256)
+            gain_plane(0, 1, t, 384, 512)
+        for n in range(4):
+            finish("scalar", 0, n, n, 0, 512)
+        gain(0, 1, 0, 256)
+        gain(0, 1, 256, 384)
+        quantize("h_01", 0, 256)
+        interleave(1, 1, 0, 256)
+        interleave(0, 1, 384, 512)
+        quantize("h_11", 0, 256)
         interleave(1, 1, 256, 512)
-        quantize("h_11")
+        quantize("h_01", 256, 512)
+        quantize("h_11", 256, 512)
+        for b, c0 in ((0, 0), (1, 0), (0, 256)):
+            for n in range(4):
+                branch_pass(b, 1, n, 4 + n, c0, c0 + 256)
         for n in range(4):
-            direct_pass(0, n, 0, 4 + n)
-            direct_pass(0, n, 1, 4 + n)
-        for n in range(4):
-            branch_pass(0, 0, n, 4 + n, 0, 512)
-        for n in range(4):
-            branch_pass(1, 0, n, 4 + n, 0, 512)
-            finish("scalar", 0, n, 4 + n, 0, 512)
-        for n in range(4):
-            direct_pass(1, n, 0, n)
-            direct_pass(1, n, 1, n)
-        for n in range(4):
-            branch_pass(0, 1, n, n, 0, 512)
-        for n in range(4):
-            branch_pass(1, 1, n, n, 0, 512)
-            finish("vector" if n % 2 else "scalar", 1, n, n, 0, 512)
+            branch_pass(1, 1, n, 4 + n, 256, 512)
+            finish("vector" if n % 2 else "scalar", 1, n, 4 + n, 0, 512)

@@ -44,7 +44,7 @@ def tile_list_meta_adapted_steps_kernel(tc, tab_words, tab_scales, offs, w1, b1,
         tab_sc = sb([P, T // 4], I32, "tab_sc")
         moved = [sb([P, COLS // 4], I32, "moved%d" % s) for s in range(2)]
         wd_sc = sb([P, 2, N // 4], I32, "wd_sc")
-        rows = sb([P, COLS], F32, "rows")
+        rows = sb([P, COLS + P], F32, "rows")
         nc.vector.memset(tab_sc[:], 0)
         nc.vector.memset(rows[:], 0.0)
         nc.vector.memset(wd_sc[:], 0)
@@ -56,6 +56,7 @@ def tile_list_meta_adapted_steps_kernel(tc, tab_words, tab_scales, offs, w1, b1,
         lr_sb = sb([P, N // P], F32, "lr_sb")
 
         def load_vectors():
+            nc.gpsimd.dma_start(out=rows[0:4, COLS : COLS + P], in_=lr.rearrange("(n p) -> n p", p=P))
             nc.sync.dma_start(out=rows[0:2, 0:COLS], in_=b1.rearrange("(b c) -> b c", b=2))
             nc.sync.dma_start(out=rows[2:4, 0:COLS], in_=g.rearrange("(b c) -> b c", b=2))
 
@@ -64,6 +65,9 @@ def tile_list_meta_adapted_steps_kernel(tc, tab_words, tab_scales, offs, w1, b1,
             for t in range(PACK):
                 nc.tensor.transpose(turned[:, t, :], rows[:, t:COLS:PACK], ident[:])
             nc.scalar.activation(out=per_r[:], in_=turned[:, :, 0:4].rearrange("p t k -> p k t"), func=COPY)
+            turned_lr = psum.tile([P, P], F32, name="turned_lr", tag="bank6")
+            nc.tensor.transpose(turned_lr[:], rows[:, COLS : COLS + P], ident[:])
+            nc.scalar.activation(out=lr_sb[:], in_=turned_lr[:, 0:4], func=COPY)
 
         def load_scale_rows(dst, src):
             for q in range(QUADS):
@@ -123,7 +127,7 @@ def tile_list_meta_adapted_steps_kernel(tc, tab_words, tab_scales, offs, w1, b1,
 
         def cast(engine, dst, src):
             if engine == "scalar":
-                nc.scalar.activation(out=dst, in_=src, func=COPY)
+                nc.scalar.copy(out=dst, in_=src)
             else:
                 nc.vector.tensor_copy(out=dst, in_=src)
 
@@ -135,8 +139,8 @@ def tile_list_meta_adapted_steps_kernel(tc, tab_words, tab_scales, offs, w1, b1,
             return rounded[key]
 
         def round_w1(engine, a, b, m0, m1):
-            dst = staged("w1_%d%d" % (a, b))[:].rearrange("p (t m j) -> p m j t", t=PACK, j=PACK)[:, m0:m1, :, :]
-            src = w1_raw[a, b][:].rearrange("p j (m t) -> p m j t", t=PACK)[:, m0:m1, :, :]
+            dst = staged("w1_%d%d" % (a, b))[:].rearrange("p (t m e j) -> p m j e t", t=PACK, e=2, j=PACK)[:, m0 // 2 : m1 // 2, :, :, :]
+            src = w1_raw[a, b][:].rearrange("p j (m e t) -> p m j e t", e=2, t=PACK)[:, m0 // 2 : m1 // 2, :, :, :]
             cast(engine, dst, src)
 
         def round_w2(engine, b, c0, c1):
@@ -228,8 +232,6 @@ def tile_list_meta_adapted_steps_kernel(tc, tab_words, tab_scales, offs, w1, b1,
         load_wd()
         load_w2(0, 0, 512)
         load_w2(1, 0, 512)
-        with nc.allow_non_contiguous_dma(reason="one rate for each partition"):
-            nc.sync.dma_start(out=lr_sb[:], in_=lr.rearrange("(n p) -> p n", p=P))
         gather_words(1, 0)
         round_w1("scalar", 1, 0, 88, 128)
         round_w1("vector", 1, 0, 0, 88)

@@ -32,8 +32,7 @@ def tile_list_meta_adapted_steps_kernel(tc, tab_words, tab_scales, offs, w1, b1,
         keep = ctx.enter_context(tc.tile_pool(name="keep", bufs=1))
         psum = ctx.enter_context(tc.psum_pool(name="psum", bufs=1))
 
-        shared = {"rounded_h_00": "w1_raw11", "rounded_h_10": "w2_raw0", "gained11": "w2_raw1", "gained01": "rounded_w2_0", "rounded_h_01": "tanh_out10", "v_codes11": "rounded_w1_10",
-                  "picked1": "tab0"}
+        shared = {"rounded_h_00": "w1_raw11", "rounded_h_10": "w2_raw0", "gained11": "w2_raw1", "rounded_h_01": "tanh_out10"}
 
         def sb(shape, dtype, name):
             return keep.tile(shape, dtype, name=name, tag=shared.get(name, name), align_bytes=64)
@@ -42,14 +41,13 @@ def tile_list_meta_adapted_steps_kernel(tc, tab_words, tab_scales, offs, w1, b1,
         nc.sync.dma_start(offsets[:], offs)
 
         tab_sc = sb([P, T // 4], I32, "tab_sc")
-        moved = [sb([P, COLS // 4], I32, "moved%d" % s) for s in range(2)]
+        moved = sb([P, S // 4], I32, "moved")
         wd_sc = sb([P, 2, N // 4], I32, "wd_sc")
         rows = sb([P, COLS + P], F32, "rows")
         nc.vector.memset(tab_sc[:], 0)
         nc.vector.memset(rows[:], 0.0)
         nc.vector.memset(wd_sc[:], 0)
-        for s in range(2):
-            nc.vector.memset(moved[s][96:P, :], 0)
+        nc.vector.memset(moved[96:P, :], 0)
         ident = sb([P, P], F32, "ident")
         make_identity(nc, ident[:])
         per_r = sb([P, 4, PACK], F32, "per_r")
@@ -107,23 +105,22 @@ def tile_list_meta_adapted_steps_kernel(tc, tab_words, tab_scales, offs, w1, b1,
 
         v_codes, v_scales = {}, {}
 
-        def lists(s):
-            return offsets[:, s * (COLS // 16) : (s + 1) * (COLS // 16)]
+        picked = sb([P, S // 4], I32, "picked")
+        for s in range(2):
+            v_scales[0, s] = picked[:].bitcast(U8)[:, s * COLS : (s + 1) * COLS]
+            v_scales[1, s] = moved[:].bitcast(U8)[:, s * COLS : (s + 1) * COLS]
 
-        picked = {}
+        def gather_scales():
+            nc.vector.tensor_copy(picked[:].bitcast(U8), tab_sc[:].bitcast(U8).indirect(offsets[:]))
 
-        def gather_scales(s):
-            picked[s] = sb([P, COLS // 4], I32, "picked%d" % s)
-            nc.vector.tensor_copy(picked[s][:].bitcast(U8), tab_sc[:].bitcast(U8).indirect(lists(s)))
-            v_scales[0, s] = picked[s][:].bitcast(U8)
-            v_scales[1, s] = moved[s][:].bitcast(U8)
+        def move_scales():
+            nc.sync.dma_start(out=moved[0:112, :], in_=picked[16:P, :])
 
-        def move_scales(s):
-            nc.sync.dma_start(out=moved[s][0:112, :], in_=picked[s][16:P, :])
-
-        def gather_words(a, s):
-            v_codes[a, s] = sb([P, COLS], U32, "v_codes%d%d" % (a, s))
-            nc.vector.tensor_copy(v_codes[a, s][:], tab[a][:].bitcast(U32).indirect(lists(s)))
+        def gather_words(a, s0, s1):
+            words = sb([P, (s1 - s0) * COLS], U32, "v_codes%d%d" % (a, s0))
+            nc.vector.tensor_copy(words[:], tab[a][:].bitcast(U32).indirect(offsets[:, s0 * (COLS // 16) : s1 * (COLS // 16)]))
+            for s in range(s0, s1):
+                v_codes[a, s] = words[:, (s - s0) * COLS : (s - s0 + 1) * COLS]
 
         def cast(engine, dst, src):
             if engine == "scalar":
@@ -166,7 +163,7 @@ def tile_list_meta_adapted_steps_kernel(tc, tab_words, tab_scales, offs, w1, b1,
             key = "w1_%d%d" % (a, b)
             cols = slice(t * P, (t + 1) * P)
             nc.tensor.matmul_mx(out=acc[:], lhsT=codes[key][:, cols].bitcast(E4M3), lhsT_scale=scales[key][:, cols],
-                                rhs=v_codes[a, s][:].bitcast(E5M2), rhs_scale=v_scales[a, s],
+                                rhs=v_codes[a, s].bitcast(E5M2), rhs_scale=v_scales[a, s],
                                 start=(a == 0), stop=(a == 1))
 
         tanh_out, gained = {}, {}
@@ -198,7 +195,7 @@ def tile_list_meta_adapted_steps_kernel(tc, tab_words, tab_scales, offs, w1, b1,
             cols = slice(n * P, (n + 1) * P)
             nc.tensor.matmul_mx(out=acc[:], lhsT=wd[:, a, cols].bitcast(E4M3),
                                 lhsT_scale=wd_sc[:, a, :].bitcast(U8)[:, cols],
-                                rhs=v_codes[a, s][:].bitcast(E5M2), rhs_scale=v_scales[a, s],
+                                rhs=v_codes[a, s].bitcast(E5M2), rhs_scale=v_scales[a, s],
                                 start=(a == 0), stop=False)
 
         def branch_pass(b, s, n, bk, c0, c1):
@@ -216,29 +213,23 @@ def tile_list_meta_adapted_steps_kernel(tc, tab_words, tab_scales, offs, w1, b1,
                 nc.vector.tensor_scalar(out=res[:], in0=banks[bk][:, c0:c1], scalar1=lr_sb[:, n : n + 1], scalar2=None, op0=MULT)
             nc.sync.dma_start(out=out[n * P : (n + 1) * P, s * COLS + c0 : s * COLS + c1], in_=res[:])
 
-        round_w1("scalar", 0, 0, 40, 128)
-        round_w1("vector", 0, 0, 0, 40)
-        gather_scales(0)
+        round_w1("scalar", 0, 0, 0, 128)
+        gather_scales()
         turn_vectors()
         quantize("w1_00")
-        gather_words(0, 0)
-        gather_words(0, 1)
-        gather_scales(1)
+        gather_words(0, 0, 1)
+        gather_words(0, 1, 2)
         load_w1(1, 0, 0, 512)
-        move_scales(0)
+        move_scales()
         load_w1(0, 1, 0, 512)
-        move_scales(1)
         load_w1(1, 1, 0, 512)
         load_wd()
         load_w2(0, 0, 512)
         load_w2(1, 0, 512)
-        gather_words(1, 0)
-        round_w1("scalar", 1, 0, 88, 128)
-        round_w1("vector", 1, 0, 0, 88)
-        quantize("w1_10", 0, 128)
-        quantize("w1_10", 128, 256)
-        quantize("w1_10", 256, 512)
-        gather_words(1, 1)
+        gather_words(1, 0, 2)
+        round_w1("scalar", 1, 0, 56, 128)
+        round_w1("vector", 1, 0, 0, 56)
+        quantize("w1_10")
         for s in range(2):
             for t in range(PACK):
                 hidden_pass(0, s, t, 0, 4 * s + t)
@@ -249,8 +240,7 @@ def tile_list_meta_adapted_steps_kernel(tc, tab_words, tab_scales, offs, w1, b1,
         round_w1("vector", 0, 1, 0, 128)
         quantize("w1_01")
         round_w1("vector", 1, 1, 0, 128)
-        quantize("w1_11", 0, 256)
-        quantize("w1_11", 256, 512)
+        quantize("w1_11")
         for s in range(2):
             for t in range(PACK):
                 hidden_pass(1, s, t, 0, 4 * s + t)
@@ -264,8 +254,15 @@ def tile_list_meta_adapted_steps_kernel(tc, tab_words, tab_scales, offs, w1, b1,
         quantize("w2_0")
         gain(1, 0, 0, 512)
         round_w2("scalar", 1, 0, 512)
+        for t in range(PACK):
+            gain_plane(1, 1, t, 0, 512)
+        gain(0, 1, 0, 512)
         quantize("h_10")
         quantize("w2_1")
+        quantize("h_01")
+        interleave(1, 1, 0, 512)
+        quantize("h_11", 0, 256)
+        quantize("h_11", 256, 512)
         for n in range(4):
             direct_pass(0, n, 0, n)
             direct_pass(0, n, 1, n)
@@ -276,25 +273,11 @@ def tile_list_meta_adapted_steps_kernel(tc, tab_words, tab_scales, offs, w1, b1,
             direct_pass(1, n, 1, 4 + n)
         for n in range(4):
             branch_pass(1, 0, n, n, 0, 512)
-        for c0 in (0, 256):
-            for t in range(PACK):
-                gain_plane(1, 1, t, c0, c0 + 256)
-        for t in range(PACK):
-            gain_plane(0, 1, t, 384, 512)
-        for n in range(4):
             finish("scalar", 0, n, n, 0, 512)
-        gain(0, 1, 0, 256)
-        gain(0, 1, 256, 384)
-        quantize("h_01", 0, 256)
-        interleave(1, 1, 0, 256)
-        interleave(0, 1, 384, 512)
-        quantize("h_11", 0, 256)
-        interleave(1, 1, 256, 512)
-        quantize("h_01", 256, 512)
-        quantize("h_11", 256, 512)
-        for b, c0 in ((0, 0), (1, 0), (0, 256)):
-            for n in range(4):
-                branch_pass(b, 1, n, 4 + n, c0, c0 + 256)
+        for n in range(4):
+            branch_pass(0, 1, n, 4 + n, 0, 512)
+        for n in range(4):
+            branch_pass(1, 1, n, 4 + n, 0, 256)
         for n in range(4):
             branch_pass(1, 1, n, 4 + n, 256, 512)
             finish("vector" if n % 2 else "scalar", 1, n, 4 + n, 0, 512)

@@ -32,7 +32,8 @@ def tile_list_meta_adapted_steps_kernel(tc, tab_words, tab_scales, offs, w1, b1,
         keep = ctx.enter_context(tc.tile_pool(name="keep", bufs=1))
         psum = ctx.enter_context(tc.psum_pool(name="psum", bufs=1))
 
-        shared = {"rounded_h_00": "w1_raw11", "rounded_h_10": "w2_raw0", "gained11": "w2_raw1", "rounded_h_01": "tanh_out10"}
+        shared = {"rounded_h_00": "w1_raw11", "rounded_h_10": "w2_raw0", "gained11": "w2_raw1", "rounded_h_01": "tanh_out10",
+                  "rounded_h_01b": "rounded_w2_1"}
 
         def sb(shape, dtype, name):
             return keep.tile(shape, dtype, name=name, tag=shared.get(name, name), align_bytes=64)
@@ -47,7 +48,7 @@ def tile_list_meta_adapted_steps_kernel(tc, tab_words, tab_scales, offs, w1, b1,
         nc.vector.memset(tab_sc[:], 0)
         nc.vector.memset(rows[:], 0.0)
         nc.vector.memset(wd_sc[:], 0)
-        nc.vector.memset(moved[96:P, :], 0)
+        nc.vector.memset(moved[:], 0)
         ident = sb([P, P], F32, "ident")
         make_identity(nc, ident[:])
         per_r = sb([P, 4, PACK], F32, "per_r")
@@ -114,7 +115,8 @@ def tile_list_meta_adapted_steps_kernel(tc, tab_words, tab_scales, offs, w1, b1,
             nc.vector.tensor_copy(picked[:].bitcast(U8), tab_sc[:].bitcast(U8).indirect(offsets[:]))
 
         def move_scales():
-            nc.sync.dma_start(out=moved[0:112, :], in_=picked[16:P, :])
+            for q in range(QUADS):
+                nc.sync.dma_start(out=moved[32 * q : 32 * q + 4, :], in_=picked[32 * q + 16 : 32 * q + 20, :])
 
         def gather_words(a, s0, s1):
             words = sb([P, (s1 - s0) * COLS], U32, "v_codes%d%d" % (a, s0))
@@ -229,7 +231,8 @@ def tile_list_meta_adapted_steps_kernel(tc, tab_words, tab_scales, offs, w1, b1,
         gather_words(1, 0, 2)
         round_w1("scalar", 1, 0, 56, 128)
         round_w1("vector", 1, 0, 0, 56)
-        quantize("w1_10")
+        quantize("w1_10", 0, 256)
+        quantize("w1_10", 256, 512)
         for s in range(2):
             for t in range(PACK):
                 hidden_pass(0, s, t, 0, 4 * s + t)
@@ -240,7 +243,8 @@ def tile_list_meta_adapted_steps_kernel(tc, tab_words, tab_scales, offs, w1, b1,
         round_w1("vector", 0, 1, 0, 128)
         quantize("w1_01")
         round_w1("vector", 1, 1, 0, 128)
-        quantize("w1_11")
+        quantize("w1_11", 0, 256)
+        quantize("w1_11", 256, 512)
         for s in range(2):
             for t in range(PACK):
                 hidden_pass(1, s, t, 0, 4 * s + t)
@@ -256,10 +260,12 @@ def tile_list_meta_adapted_steps_kernel(tc, tab_words, tab_scales, offs, w1, b1,
         round_w2("scalar", 1, 0, 512)
         for t in range(PACK):
             gain_plane(1, 1, t, 0, 512)
-        gain(0, 1, 0, 512)
         quantize("h_10")
+        gain(0, 1, 0, 256)
         quantize("w2_1")
-        quantize("h_01")
+        quantize("h_01", 0, 256)
+        gain(0, 1, 256, 512, "b")
+        quantize("h_01", 256, 512, "b")
         interleave(1, 1, 0, 512)
         quantize("h_11", 0, 256)
         quantize("h_11", 256, 512)
@@ -274,10 +280,9 @@ def tile_list_meta_adapted_steps_kernel(tc, tab_words, tab_scales, offs, w1, b1,
         for n in range(4):
             branch_pass(1, 0, n, n, 0, 512)
             finish("scalar", 0, n, n, 0, 512)
-        for n in range(4):
-            branch_pass(0, 1, n, 4 + n, 0, 512)
-        for n in range(4):
-            branch_pass(1, 1, n, 4 + n, 0, 256)
+        for b, c0 in ((0, 0), (0, 256), (1, 0)):
+            for n in range(4):
+                branch_pass(b, 1, n, 4 + n, c0, c0 + 256)
         for n in range(4):
             branch_pass(1, 1, n, 4 + n, 256, 512)
             finish("vector" if n % 2 else "scalar", 1, n, 4 + n, 0, 512)

@@ -17,13 +17,27 @@ E5M2 = mybir.dt.float8_e5m2_x4
 TANH = mybir.ActivationFunctionType.Tanh
 COPY = mybir.ActivationFunctionType.Copy
 MULT = mybir.AluOpType.mult
-ADD = mybir.AluOpType.add
 
 P = 128
 PACK = 4
 PASS = P * PACK
 COLS = 512
+MID = COLS // 2
 QUADS = 4
+LOWER = 16
+GROUP = 16
+OUT_TILES = N // P
+
+VECTOR_SHARE_10 = 16
+VECTOR_SHARE_01 = 68
+
+SAME_BYTES = {
+    "rounded_h_00": "w1_raw11",
+    "rounded_h_10": "w2_raw0",
+    "gained11": "w2_raw1",
+    "rounded_h_01": "tanh_out10",
+    "rounded_h_01b": "rounded_w2_1",
+}
 
 
 def tile_list_meta_adapted_steps_kernel(tc, tab_words, tab_scales, offs, w1, b1, g, w2, wd_words, wd_scales, lr, out):
@@ -32,13 +46,10 @@ def tile_list_meta_adapted_steps_kernel(tc, tab_words, tab_scales, offs, w1, b1,
         keep = ctx.enter_context(tc.tile_pool(name="keep", bufs=1))
         psum = ctx.enter_context(tc.psum_pool(name="psum", bufs=1))
 
-        shared = {"rounded_h_00": "w1_raw11", "rounded_h_10": "w2_raw0", "gained11": "w2_raw1", "rounded_h_01": "tanh_out10",
-                  "rounded_h_01b": "rounded_w2_1"}
-
         def sb(shape, dtype, name):
-            return keep.tile(shape, dtype, name=name, tag=shared.get(name, name), align_bytes=64)
+            return keep.tile(shape, dtype, name=name, tag=SAME_BYTES.get(name, name), align_bytes=64)
 
-        offsets = keep.tile([P, S // 16], U16, name="offsets")
+        offsets = keep.tile([P, S // GROUP], U16, name="offsets")
         nc.sync.dma_start(offsets[:], offs)
 
         tab_sc = sb([P, T // 4], I32, "tab_sc")
@@ -52,10 +63,10 @@ def tile_list_meta_adapted_steps_kernel(tc, tab_words, tab_scales, offs, w1, b1,
         ident = sb([P, P], F32, "ident")
         make_identity(nc, ident[:])
         per_r = sb([P, 4, PACK], F32, "per_r")
-        lr_sb = sb([P, N // P], F32, "lr_sb")
+        lr_sb = sb([P, OUT_TILES], F32, "lr_sb")
 
         def load_vectors():
-            nc.gpsimd.dma_start(out=rows[0:4, COLS : COLS + P], in_=lr.rearrange("(n p) -> n p", p=P))
+            nc.gpsimd.dma_start(out=rows[0:OUT_TILES, COLS : COLS + P], in_=lr.rearrange("(n p) -> n p", p=P))
             nc.sync.dma_start(out=rows[0:2, 0:COLS], in_=b1.rearrange("(b c) -> b c", b=2))
             nc.sync.dma_start(out=rows[2:4, 0:COLS], in_=g.rearrange("(b c) -> b c", b=2))
 
@@ -66,12 +77,12 @@ def tile_list_meta_adapted_steps_kernel(tc, tab_words, tab_scales, offs, w1, b1,
             nc.scalar.activation(out=per_r[:], in_=turned[:, :, 0:4].rearrange("p t k -> p k t"), func=COPY)
             turned_lr = psum.tile([P, P], F32, name="turned_lr", tag="bank6")
             nc.tensor.transpose(turned_lr[:], rows[:, COLS : COLS + P], ident[:])
-            nc.scalar.activation(out=lr_sb[:], in_=turned_lr[:, 0:4], func=COPY)
+            nc.scalar.activation(out=lr_sb[:], in_=turned_lr[:, 0:OUT_TILES], func=COPY)
 
-        def load_scale_rows(dst, src):
+        def load_wd_scales():
             for q in range(QUADS):
-                nc.gpsimd.dma_start(out=dst[32 * q : 32 * q + 4, :, :],
-                                  in_=src[:, 4 * q : 4 * q + 4, :].bitcast(I32).rearrange("a r c -> r a c"))
+                nc.gpsimd.dma_start(out=wd_sc[32 * q : 32 * q + 4, :, :],
+                                    in_=wd_scales[:, 4 * q : 4 * q + 4, :].bitcast(I32).rearrange("a r c -> r a c"))
 
         tab = [sb([P, T], I32, "tab%d" % a) for a in range(2)]
         w1_raw = {(a, b): sb([P, PACK, COLS], F32, "w1_raw%d%d" % (a, b)) for a in range(2) for b in range(2)}
@@ -81,26 +92,26 @@ def tile_list_meta_adapted_steps_kernel(tc, tab_words, tab_scales, offs, w1, b1,
         def load_tab(a):
             nc.sync.dma_start(out=tab[a][:], in_=tab_words[a].rearrange("p c i -> p (c i)").bitcast(I32))
 
-        def load_w1(a, b, c0, c1):
-            rows = w1[a * PASS : (a + 1) * PASS, b * COLS + c0 : b * COLS + c1]
-            nc.sync.dma_start(out=w1_raw[a, b][:, :, c0:c1], in_=rows.rearrange("(p j) c -> p j c", j=PACK))
+        def load_w1(a, b):
+            part = w1[a * PASS : (a + 1) * PASS, b * COLS : (b + 1) * COLS]
+            nc.sync.dma_start(out=w1_raw[a, b][:], in_=part.rearrange("(p j) c -> p j c", j=PACK))
 
-        def load_w2(b, c0, c1):
-            rows = w2[b * PASS : (b + 1) * PASS, c0:c1]
-            nc.sync.dma_start(out=w2_raw[b][:, :, c0:c1], in_=rows.rearrange("(p j) c -> p j c", j=PACK))
+        def load_w2(b):
+            part = w2[b * PASS : (b + 1) * PASS, :]
+            nc.sync.dma_start(out=w2_raw[b][:], in_=part.rearrange("(p j) c -> p j c", j=PACK))
 
         def load_tab_scales():
             by_row = tab_scales.bitcast(I32).rearrange("a (q r) c -> r q a c", r=4)
             for r in range(4):
-                nc.sync.dma_start(out=tab_sc[r:P:16, :], in_=by_row[r])
+                nc.sync.dma_start(out=tab_sc[r:P:LOWER, :], in_=by_row[r])
 
         def load_wd():
             nc.sync.dma_start(out=wd[:], in_=wd_words.rearrange("a p c i -> p a (c i)").bitcast(I32))
 
-        load_w1(0, 0, 0, 512)
+        load_w1(0, 0)
         load_tab_scales()
         load_vectors()
-        load_scale_rows(wd_sc, wd_scales)
+        load_wd_scales()
         load_tab(0)
         load_tab(1)
 
@@ -116,11 +127,12 @@ def tile_list_meta_adapted_steps_kernel(tc, tab_words, tab_scales, offs, w1, b1,
 
         def move_scales():
             for q in range(QUADS):
-                nc.sync.dma_start(out=moved[32 * q : 32 * q + 4, :], in_=picked[32 * q + 16 : 32 * q + 20, :])
+                nc.sync.dma_start(out=moved[32 * q : 32 * q + 4, :], in_=picked[32 * q + LOWER : 32 * q + LOWER + 4, :])
 
         def gather_words(a, s0, s1):
             words = sb([P, (s1 - s0) * COLS], U32, "v_codes%d%d" % (a, s0))
-            nc.vector.tensor_copy(words[:], tab[a][:].bitcast(U32).indirect(offsets[:, s0 * (COLS // 16) : s1 * (COLS // 16)]))
+            entries = offsets[:, s0 * (COLS // GROUP) : s1 * (COLS // GROUP)]
+            nc.vector.tensor_copy(words[:], tab[a][:].bitcast(U32).indirect(entries))
             for s in range(s0, s1):
                 v_codes[a, s] = words[:, (s - s0) * COLS : (s - s0 + 1) * COLS]
 
@@ -138,13 +150,14 @@ def tile_list_meta_adapted_steps_kernel(tc, tab_words, tab_scales, offs, w1, b1,
             return rounded[key]
 
         def round_w1(engine, a, b, m0, m1):
-            dst = staged("w1_%d%d" % (a, b))[:].rearrange("p (t m e j) -> p m j e t", t=PACK, e=2, j=PACK)[:, m0 // 2 : m1 // 2, :, :, :]
-            src = w1_raw[a, b][:].rearrange("p j (m e t) -> p m j e t", e=2, t=PACK)[:, m0 // 2 : m1 // 2, :, :, :]
-            cast(engine, dst, src)
+            pairs = slice(m0 // 2, m1 // 2)
+            dst = staged("w1_%d%d" % (a, b))[:].rearrange("p (t m e j) -> p m j e t", t=PACK, e=2, j=PACK)
+            src = w1_raw[a, b][:].rearrange("p j (m e t) -> p m j e t", e=2, t=PACK)
+            cast(engine, dst[:, pairs, :, :, :], src[:, pairs, :, :, :])
 
-        def round_w2(engine, b, c0, c1):
-            dst = staged("w2_%d" % b)[:].rearrange("p (c e j) -> p c j e", e=2, j=PACK)[:, c0 // 2 : c1 // 2, :, :]
-            src = w2_raw[b][:].rearrange("p j (c e) -> p c j e", e=2)[:, c0 // 2 : c1 // 2, :, :]
+        def round_w2(engine, b):
+            dst = staged("w2_%d" % b)[:].rearrange("p (c e j) -> p c j e", e=2, j=PACK)
+            src = w2_raw[b][:].rearrange("p j (c e) -> p c j e", e=2)
             cast(engine, dst, src)
 
         def quantize(key, c0=0, c1=COLS, part=""):
@@ -156,133 +169,137 @@ def tile_list_meta_adapted_steps_kernel(tc, tab_words, tab_scales, offs, w1, b1,
 
         banks = {}
 
-        def bank(i):
-            banks[i] = psum.tile([P, COLS], F32, name="bank%d" % i, tag="bank%d" % i)
-            return banks[i]
+        def opened(s, i):
+            bk = 4 * s + i
+            banks[s, i] = psum.tile([P, COLS], F32, name="bank%d" % bk, tag="bank%d" % bk)
+            return banks[s, i]
 
-        def hidden_pass(b, s, t, a, bk):
-            acc = bank(bk) if a == 0 else banks[bk]
+        def hidden_pass(b, s, t, a):
+            acc = opened(s, t) if a == 0 else banks[s, t]
             key = "w1_%d%d" % (a, b)
             cols = slice(t * P, (t + 1) * P)
             nc.tensor.matmul_mx(out=acc[:], lhsT=codes[key][:, cols].bitcast(E4M3), lhsT_scale=scales[key][:, cols],
                                 rhs=v_codes[a, s].bitcast(E5M2), rhs_scale=v_scales[a, s],
                                 start=(a == 0), stop=(a == 1))
 
-        tanh_out, gained = {}, {}
+        tanh_out = {}
 
-        def tanh_tile(b, s, t, bk):
+        def tanh_plane(b, s, t):
             if (b, s) not in tanh_out:
                 tanh_out[b, s] = sb([P, PACK, COLS], F32, "tanh_out%d%d" % (b, s))
-            nc.scalar.activation(out=tanh_out[b, s][:, t, :], in_=banks[bk][:], func=TANH, bias=per_r[:, b, t : t + 1])
+            nc.scalar.activation(out=tanh_out[b, s][:, t, :], in_=banks[s, t][:], func=TANH, bias=per_r[:, b, t : t + 1])
 
-        def gain(b, s, c0, c1, part=""):
-            dst = staged("h_%d%d" % (b, s) + part)[:].rearrange("p (c e t) -> p c t e", e=2, t=PACK)[:, c0 // 2 : c1 // 2, :, :]
-            src = tanh_out[b, s][:].rearrange("p t (c e) -> p c t e", e=2)[:, c0 // 2 : c1 // 2, :, :]
+        def gain(b, s, c0=0, c1=COLS, part=""):
+            pairs = slice(c0 // 2, c1 // 2)
+            dst = staged("h_%d%d" % (b, s) + part)[:].rearrange("p (c e t) -> p c t e", e=2, t=PACK)
+            src = tanh_out[b, s][:].rearrange("p t (c e) -> p c t e", e=2)
             gains = per_r[:, 2 + b, :].unsqueeze(1).unsqueeze(3).to_broadcast([P, (c1 - c0) // 2, PACK, 2])
-            nc.vector.tensor_tensor(out=dst, in0=src, in1=gains, op=MULT)
+            nc.vector.tensor_tensor(out=dst[:, pairs, :, :], in0=src[:, pairs, :, :], in1=gains, op=MULT)
 
-        def gain_plane(b, s, t, c0, c1):
-            if (b, s) not in gained:
-                gained[b, s] = sb([P, PACK, COLS], BF16, "gained%d%d" % (b, s))
-            nc.scalar.activation(out=gained[b, s][:, t, c0:c1], in_=tanh_out[b, s][:, t, c0:c1], func=COPY,
-                                 scale=per_r[:, 2 + b, t : t + 1])
+        def gain_by_planes(b, s):
+            gained = sb([P, PACK, COLS], BF16, "gained%d%d" % (b, s))
+            for t in range(PACK):
+                nc.scalar.activation(out=gained[:, t, :], in_=tanh_out[b, s][:, t, :], func=COPY,
+                                     scale=per_r[:, 2 + b, t : t + 1])
+            return gained
 
-        def interleave(b, s, c0, c1):
-            dst = staged("h_%d%d" % (b, s))[:].rearrange("p (c e t) -> p c t e", e=4, t=PACK)[:, c0 // 4 : c1 // 4, :, :]
-            src = gained[b, s][:].rearrange("p t (c e) -> p c t e", e=4)[:, c0 // 4 : c1 // 4, :, :]
-            nc.vector.tensor_copy(out=dst, in_=src)
+        def interleave(b, s, gained):
+            dst = staged("h_%d%d" % (b, s))[:].rearrange("p (c e t) -> p c t e", e=4, t=PACK)
+            nc.vector.tensor_copy(out=dst, in_=gained[:].rearrange("p t (c e) -> p c t e", e=4))
 
-        def direct_pass(s, n, a, bk):
-            acc = bank(bk) if a == 0 else banks[bk]
+        def direct_passes(s, n):
+            acc = opened(s, n)
             cols = slice(n * P, (n + 1) * P)
-            nc.tensor.matmul_mx(out=acc[:], lhsT=wd[:, a, cols].bitcast(E4M3),
-                                lhsT_scale=wd_sc[:, a, :].bitcast(U8)[:, cols],
-                                rhs=v_codes[a, s].bitcast(E5M2), rhs_scale=v_scales[a, s],
-                                start=(a == 0), stop=False)
+            for a in range(2):
+                nc.tensor.matmul_mx(out=acc[:], lhsT=wd[:, a, cols].bitcast(E4M3),
+                                    lhsT_scale=wd_sc[:, a, :].bitcast(U8)[:, cols],
+                                    rhs=v_codes[a, s].bitcast(E5M2), rhs_scale=v_scales[a, s],
+                                    start=(a == 0), stop=False)
 
-        def branch_pass(b, s, n, bk, c0, c1):
+        def branch_pass(b, s, n, c0=0, c1=COLS):
             cols = slice(n * P, (n + 1) * P)
             wk, hk = "w2_%d" % b, "h_%d%d" % (b, s)
-            nc.tensor.matmul_mx(out=banks[bk][:, c0:c1], lhsT=codes[wk][:, cols].bitcast(E4M3), lhsT_scale=scales[wk][:, cols],
+            nc.tensor.matmul_mx(out=banks[s, n][:, c0:c1], lhsT=codes[wk][:, cols].bitcast(E4M3), lhsT_scale=scales[wk][:, cols],
                                 rhs=codes[hk][:, c0:c1].bitcast(E4M3), rhs_scale=scales[hk][:, c0:c1],
                                 start=False, stop=(b == 1 and c1 == COLS))
 
-        def finish(engine, s, n, bk, c0, c1):
-            res = sb([P, c1 - c0], F32, "res%d%d_%d" % (s, n, c0))
+        def finish(engine, s, n):
+            res = sb([P, COLS], F32, "res%d%d_0" % (s, n))
             if engine == "scalar":
-                nc.scalar.activation(out=res[:], in_=banks[bk][:, c0:c1], func=COPY, scale=lr_sb[:, n : n + 1])
+                nc.scalar.activation(out=res[:], in_=banks[s, n][:], func=COPY, scale=lr_sb[:, n : n + 1])
             else:
-                nc.vector.tensor_scalar(out=res[:], in0=banks[bk][:, c0:c1], scalar1=lr_sb[:, n : n + 1], scalar2=None, op0=MULT)
-            nc.sync.dma_start(out=out[n * P : (n + 1) * P, s * COLS + c0 : s * COLS + c1], in_=res[:])
+                nc.vector.tensor_scalar(out=res[:], in0=banks[s, n][:], scalar1=lr_sb[:, n : n + 1], scalar2=None, op0=MULT)
+            nc.sync.dma_start(out=out[n * P : (n + 1) * P, s * COLS : (s + 1) * COLS], in_=res[:])
 
-        round_w1("scalar", 0, 0, 0, 128)
+        round_w1("scalar", 0, 0, 0, P)
         gather_scales()
         turn_vectors()
         quantize("w1_00")
         gather_words(0, 0, 1)
         gather_words(0, 1, 2)
-        load_w1(1, 0, 0, 512)
+        load_w1(1, 0)
+        load_w1(0, 1)
         move_scales()
-        load_w1(0, 1, 0, 512)
-        load_w1(1, 1, 0, 512)
+        load_w1(1, 1)
         load_wd()
-        load_w2(0, 0, 512)
-        load_w2(1, 0, 512)
+        load_w2(0)
+        load_w2(1)
         gather_words(1, 0, 2)
-        round_w1("scalar", 1, 0, 56, 128)
-        round_w1("vector", 1, 0, 0, 56)
-        quantize("w1_10", 0, 256)
-        quantize("w1_10", 256, 512)
+        round_w1("scalar", 1, 0, VECTOR_SHARE_10, P)
+        round_w1("vector", 1, 0, 0, VECTOR_SHARE_10)
+        quantize("w1_10", 0, MID)
+        quantize("w1_10", MID, COLS)
+        round_w1("scalar", 0, 1, VECTOR_SHARE_01, P)
+        round_w1("vector", 0, 1, 0, VECTOR_SHARE_01)
+
         for s in range(2):
             for t in range(PACK):
-                hidden_pass(0, s, t, 0, 4 * s + t)
+                hidden_pass(0, s, t, 0)
         for s in range(2):
             for t in range(PACK):
-                hidden_pass(0, s, t, 1, 4 * s + t)
-                tanh_tile(0, s, t, 4 * s + t)
-        round_w1("vector", 0, 1, 0, 128)
+                hidden_pass(0, s, t, 1)
+                tanh_plane(0, s, t)
+
         quantize("w1_01")
-        round_w1("vector", 1, 1, 0, 128)
-        quantize("w1_11", 0, 256)
-        quantize("w1_11", 256, 512)
+        round_w1("vector", 1, 1, 0, P)
+        quantize("w1_11", 0, MID)
+        quantize("w1_11", MID, COLS)
         for s in range(2):
             for t in range(PACK):
-                hidden_pass(1, s, t, 0, 4 * s + t)
-        for s in range(2):
+                hidden_pass(1, s, t, 0)
             for t in range(PACK):
-                hidden_pass(1, s, t, 1, 4 * s + t)
-                tanh_tile(1, s, t, 4 * s + t)
-        gain(0, 0, 0, 512)
-        round_w2("vector", 0, 0, 512)
+                hidden_pass(1, s, t, 1)
+                tanh_plane(1, s, t)
+
+        gain(0, 0)
+        round_w2("vector", 0)
         quantize("h_00")
         quantize("w2_0")
-        gain(1, 0, 0, 512)
-        round_w2("scalar", 1, 0, 512)
-        for t in range(PACK):
-            gain_plane(1, 1, t, 0, 512)
+        gain(1, 0)
+        round_w2("scalar", 1)
+        gained_11 = gain_by_planes(1, 1)
         quantize("h_10")
-        gain(0, 1, 0, 256)
+        gain(0, 1, 0, MID)
         quantize("w2_1")
-        quantize("h_01", 0, 256)
-        gain(0, 1, 256, 512, "b")
-        quantize("h_01", 256, 512, "b")
-        interleave(1, 1, 0, 512)
-        quantize("h_11", 0, 256)
-        quantize("h_11", 256, 512)
-        for n in range(4):
-            direct_pass(0, n, 0, n)
-            direct_pass(0, n, 1, n)
-        for n in range(4):
-            branch_pass(0, 0, n, n, 0, 512)
-        for n in range(4):
-            direct_pass(1, n, 0, 4 + n)
-            direct_pass(1, n, 1, 4 + n)
-        for n in range(4):
-            branch_pass(1, 0, n, n, 0, 512)
-            finish("scalar", 0, n, n, 0, 512)
-        for b, c0 in ((0, 0), (0, 256), (1, 0)):
-            for n in range(4):
-                branch_pass(b, 1, n, 4 + n, c0, c0 + 256)
-        for n in range(4):
-            branch_pass(1, 1, n, 4 + n, 256, 512)
-            finish("vector" if n % 2 else "scalar", 1, n, 4 + n, 0, 512)
+        quantize("h_01", 0, MID)
+        gain(0, 1, MID, COLS, "b")
+        quantize("h_01", MID, COLS, "b")
+        interleave(1, 1, gained_11)
+        quantize("h_11", 0, MID)
+        quantize("h_11", MID, COLS)
+
+        for n in range(OUT_TILES):
+            direct_passes(0, n)
+        for n in range(OUT_TILES):
+            branch_pass(0, 0, n)
+        for n in range(OUT_TILES):
+            direct_passes(1, n)
+        for n in range(OUT_TILES):
+            branch_pass(1, 0, n)
+            finish("scalar", 0, n)
+        for b, c0 in ((0, 0), (0, MID), (1, 0)):
+            for n in range(OUT_TILES):
+                branch_pass(b, 1, n, c0, c0 + MID)
+        for n in range(OUT_TILES):
+            branch_pass(1, 1, n, MID, COLS)
+            finish("vector" if n % 2 else "scalar", 1, n)

@@ -1,7 +1,6 @@
 from contextlib import ExitStack
 
 import concourse.mybir as mybir
-from concourse.masks import make_identity
 
 K, T, S, H, N = 1024, 2048, 1024, 1024, 512
 FLOPS = 2 * S * (K * H + H * N + K * N)
@@ -28,14 +27,14 @@ LOWER = 16
 GROUP = 16
 OUT_TILES = N // P
 
-VECTOR_SHARE_10 = 16
-VECTOR_SHARE_01 = 68
+VECTOR_SHARE_00 = 64
+VECTOR_SHARE_10 = 64
 
 SAME_BYTES = {
-    "rounded_h_00": "w1_raw11",
+    "rounded_h_00": "w1_raw01",
+    "rounded_h_00b": "w1_raw11",
     "rounded_h_10": "w2_raw0",
-    "gained11": "w2_raw1",
-    "rounded_h_01": "tanh_out10",
+    "gained11a": "w2_raw1",
     "rounded_h_01b": "rounded_w2_1",
 }
 
@@ -55,29 +54,19 @@ def tile_list_meta_adapted_steps_kernel(tc, tab_words, tab_scales, offs, w1, b1,
         tab_sc = sb([P, T // 4], I32, "tab_sc")
         moved = sb([P, S // 4], I32, "moved")
         wd_sc = sb([P, 2, N // 4], I32, "wd_sc")
-        rows = sb([P, COLS + P], F32, "rows")
         nc.vector.memset(tab_sc[:], 0)
-        nc.vector.memset(rows[:], 0.0)
         nc.vector.memset(wd_sc[:], 0)
         nc.vector.memset(moved[:], 0)
-        ident = sb([P, P], F32, "ident")
-        make_identity(nc, ident[:])
-        per_r = sb([P, 4, PACK], F32, "per_r")
-        lr_sb = sb([P, OUT_TILES], F32, "lr_sb")
+        per_r = sb([P, 4, 8], F32, "per_r")
+        lr_sb = sb([P, OUT_TILES, 8], F32, "lr_sb")
 
         def load_vectors():
-            nc.gpsimd.dma_start(out=rows[0:OUT_TILES, COLS : COLS + P], in_=lr.rearrange("(n p) -> n p", p=P))
-            nc.sync.dma_start(out=rows[0:2, 0:COLS], in_=b1.rearrange("(b c) -> b c", b=2))
-            nc.sync.dma_start(out=rows[2:4, 0:COLS], in_=g.rearrange("(b c) -> b c", b=2))
+            nc.gpsimd.dma_start(out=per_r[:, 0:2, 0:PACK], in_=b1.rearrange("(b p t) -> p b t", b=2, t=PACK))
+            nc.gpsimd.dma_start(out=per_r[:, 2:4, 0:PACK], in_=g.rearrange("(b p t) -> p b t", b=2, t=PACK))
 
-        def turn_vectors():
-            turned = psum.tile([P, PACK, P], F32, name="turned", tag="bank7")
-            for t in range(PACK):
-                nc.tensor.transpose(turned[:, t, :], rows[:, t:COLS:PACK], ident[:])
-            nc.scalar.activation(out=per_r[:], in_=turned[:, :, 0:4].rearrange("p t k -> p k t"), func=COPY)
-            turned_lr = psum.tile([P, P], F32, name="turned_lr", tag="bank6")
-            nc.tensor.transpose(turned_lr[:], rows[:, COLS : COLS + P], ident[:])
-            nc.scalar.activation(out=lr_sb[:], in_=turned_lr[:, 0:OUT_TILES], func=COPY)
+        def load_lr():
+            with nc.allow_non_contiguous_dma(reason="one rate for each partition and output tile"):
+                nc.sync.dma_start(out=lr_sb[:, :, 0:1], in_=lr.rearrange("(n p o) -> p n o", p=P, o=1))
 
         def load_wd_scales():
             for q in range(QUADS):
@@ -108,12 +97,12 @@ def tile_list_meta_adapted_steps_kernel(tc, tab_words, tab_scales, offs, w1, b1,
         def load_wd():
             nc.sync.dma_start(out=wd[:], in_=wd_words.rearrange("a p c i -> p a (c i)").bitcast(I32))
 
+        load_vectors()
         load_w1(0, 0)
         load_tab_scales()
-        load_vectors()
         load_wd_scales()
         load_tab(0)
-        load_tab(1)
+        load_w1(1, 0)
 
         v_codes, v_scales = {}, {}
 
@@ -126,8 +115,7 @@ def tile_list_meta_adapted_steps_kernel(tc, tab_words, tab_scales, offs, w1, b1,
             nc.vector.tensor_copy(picked[:].bitcast(U8), tab_sc[:].bitcast(U8).indirect(offsets[:]))
 
         def move_scales():
-            for q in range(QUADS):
-                nc.sync.dma_start(out=moved[32 * q : 32 * q + 4, :], in_=picked[32 * q + LOWER : 32 * q + LOWER + 4, :])
+            nc.sync.dma_start(out=moved[0 : P - LOWER, :], in_=picked[LOWER:P, :])
 
         def gather_words(a, s0, s1):
             words = sb([P, (s1 - s0) * COLS], U32, "v_codes%d%d" % (a, s0))
@@ -193,18 +181,18 @@ def tile_list_meta_adapted_steps_kernel(tc, tab_words, tab_scales, offs, w1, b1,
             pairs = slice(c0 // 2, c1 // 2)
             dst = staged("h_%d%d" % (b, s) + part)[:].rearrange("p (c e t) -> p c t e", e=2, t=PACK)
             src = tanh_out[b, s][:].rearrange("p t (c e) -> p c t e", e=2)
-            gains = per_r[:, 2 + b, :].unsqueeze(1).unsqueeze(3).to_broadcast([P, (c1 - c0) // 2, PACK, 2])
+            gains = per_r[:, 2 + b, 0:PACK].unsqueeze(1).unsqueeze(3).to_broadcast([P, (c1 - c0) // 2, PACK, 2])
             nc.vector.tensor_tensor(out=dst[:, pairs, :, :], in0=src[:, pairs, :, :], in1=gains, op=MULT)
 
-        def gain_by_planes(b, s):
-            gained = sb([P, PACK, COLS], BF16, "gained%d%d" % (b, s))
+        def gain_by_planes(b, s, c0, c1, part):
+            gained = sb([P, PACK, c1 - c0], BF16, "gained%d%d" % (b, s) + part)
             for t in range(PACK):
-                nc.scalar.activation(out=gained[:, t, :], in_=tanh_out[b, s][:, t, :], func=COPY,
+                nc.scalar.activation(out=gained[:, t, :], in_=tanh_out[b, s][:, t, c0:c1], func=COPY,
                                      scale=per_r[:, 2 + b, t : t + 1])
             return gained
 
-        def interleave(b, s, gained):
-            dst = staged("h_%d%d" % (b, s))[:].rearrange("p (c e t) -> p c t e", e=4, t=PACK)
+        def interleave(b, s, gained, c0, c1):
+            dst = staged("h_%d%d" % (b, s))[:, PACK * c0 : PACK * c1].rearrange("p (c e t) -> p c t e", e=4, t=PACK)
             nc.vector.tensor_copy(out=dst, in_=gained[:].rearrange("p t (c e) -> p c t e", e=4))
 
         def direct_passes(s, n):
@@ -226,31 +214,35 @@ def tile_list_meta_adapted_steps_kernel(tc, tab_words, tab_scales, offs, w1, b1,
         def finish(engine, s, n):
             res = sb([P, COLS], F32, "res%d%d_0" % (s, n))
             if engine == "scalar":
-                nc.scalar.activation(out=res[:], in_=banks[s, n][:], func=COPY, scale=lr_sb[:, n : n + 1])
+                nc.scalar.activation(out=res[:], in_=banks[s, n][:], func=COPY, scale=lr_sb[:, n, 0:1])
             else:
-                nc.vector.tensor_scalar(out=res[:], in0=banks[s, n][:], scalar1=lr_sb[:, n : n + 1], scalar2=None, op0=MULT)
+                nc.vector.tensor_scalar(out=res[:], in0=banks[s, n][:], scalar1=lr_sb[:, n, 0:1], scalar2=None, op0=MULT)
             nc.sync.dma_start(out=out[n * P : (n + 1) * P, s * COLS : (s + 1) * COLS], in_=res[:])
 
-        round_w1("scalar", 0, 0, 0, P)
+        round_w1("scalar", 0, 0, VECTOR_SHARE_00, P)
+        round_w1("vector", 0, 0, 0, VECTOR_SHARE_00)
         gather_scales()
-        turn_vectors()
-        quantize("w1_00")
-        gather_words(0, 0, 1)
-        gather_words(0, 1, 2)
-        load_w1(1, 0)
-        load_w1(0, 1)
+        load_tab(1)
         move_scales()
+        load_w1(0, 1)
         load_w1(1, 1)
         load_wd()
         load_w2(0)
         load_w2(1)
-        gather_words(1, 0, 2)
+        load_lr()
+        quantize("w1_00")
+        gather_words(0, 0, 1)
+        gather_words(0, 1, 2)
         round_w1("scalar", 1, 0, VECTOR_SHARE_10, P)
         round_w1("vector", 1, 0, 0, VECTOR_SHARE_10)
-        quantize("w1_10", 0, MID)
-        quantize("w1_10", MID, COLS)
-        round_w1("scalar", 0, 1, VECTOR_SHARE_01, P)
-        round_w1("vector", 0, 1, 0, VECTOR_SHARE_01)
+        quantize("w1_10")
+        gather_words(1, 0, 1)
+        gather_words(1, 1, 2)
+        round_w1("vector", 0, 1, 0, P)
+        quantize("w1_01")
+        round_w1("vector", 1, 1, 0, P)
+        quantize("w1_11", 0, MID)
+        quantize("w1_11", MID, COLS)
 
         for s in range(2):
             for t in range(PACK):
@@ -259,33 +251,34 @@ def tile_list_meta_adapted_steps_kernel(tc, tab_words, tab_scales, offs, w1, b1,
             for t in range(PACK):
                 hidden_pass(0, s, t, 1)
                 tanh_plane(0, s, t)
-
-        quantize("w1_01")
-        round_w1("vector", 1, 1, 0, P)
-        quantize("w1_11", 0, MID)
-        quantize("w1_11", MID, COLS)
         for s in range(2):
             for t in range(PACK):
                 hidden_pass(1, s, t, 0)
+        for s in range(2):
             for t in range(PACK):
                 hidden_pass(1, s, t, 1)
                 tanh_plane(1, s, t)
 
-        gain(0, 0)
+        gain(0, 0, 0, MID)
+        gain(0, 0, MID, COLS, "b")
+        gained_01a = gain_by_planes(0, 1, 0, MID, "a")
         round_w2("vector", 0)
-        quantize("h_00")
+        quantize("h_00", 0, MID)
+        quantize("h_00", MID, COLS, "b")
         quantize("w2_0")
         gain(1, 0)
         round_w2("scalar", 1)
-        gained_11 = gain_by_planes(1, 1)
+        gained_11a = gain_by_planes(1, 1, 0, MID, "a")
+        gained_11b = gain_by_planes(1, 1, MID, COLS, "b")
+        interleave(0, 1, gained_01a, 0, MID)
         quantize("h_10")
-        gain(0, 1, 0, MID)
         quantize("w2_1")
         quantize("h_01", 0, MID)
         gain(0, 1, MID, COLS, "b")
+        interleave(1, 1, gained_11a, 0, MID)
         quantize("h_01", MID, COLS, "b")
-        interleave(1, 1, gained_11)
         quantize("h_11", 0, MID)
+        interleave(1, 1, gained_11b, MID, COLS)
         quantize("h_11", MID, COLS)
 
         for n in range(OUT_TILES):

@@ -27,14 +27,13 @@ LOWER = 16
 GROUP = 16
 OUT_TILES = N // P
 
-VECTOR_SHARE_00 = 64
-VECTOR_SHARE_10 = 64
+VECTOR_SHARE_10 = 32
 
 SAME_BYTES = {
     "rounded_h_00": "w1_raw01",
     "rounded_h_00b": "w1_raw11",
     "rounded_h_10": "w2_raw0",
-    "gained11a": "w2_raw1",
+    "gained11b": "w2_raw1",
     "rounded_h_01b": "rounded_w2_1",
 }
 
@@ -61,17 +60,17 @@ def tile_list_meta_adapted_steps_kernel(tc, tab_words, tab_scales, offs, w1, b1,
         lr_sb = sb([P, OUT_TILES, 8], F32, "lr_sb")
 
         def load_vectors():
-            nc.gpsimd.dma_start(out=per_r[:, 0:2, 0:PACK], in_=b1.rearrange("(b p t) -> p b t", b=2, t=PACK))
-            nc.gpsimd.dma_start(out=per_r[:, 2:4, 0:PACK], in_=g.rearrange("(b p t) -> p b t", b=2, t=PACK))
+            nc.scalar.dma_start(out=per_r[:, 0:2, 0:PACK], in_=b1.rearrange("(b p t) -> p b t", b=2, t=PACK))
+            nc.scalar.dma_start(out=per_r[:, 2:4, 0:PACK], in_=g.rearrange("(b p t) -> p b t", b=2, t=PACK))
 
         def load_lr():
             with nc.allow_non_contiguous_dma(reason="one rate for each partition and output tile"):
                 nc.sync.dma_start(out=lr_sb[:, :, 0:1], in_=lr.rearrange("(n p o) -> p n o", p=P, o=1))
 
         def load_wd_scales():
-            for q in range(QUADS):
-                nc.gpsimd.dma_start(out=wd_sc[32 * q : 32 * q + 4, :, :],
-                                    in_=wd_scales[:, 4 * q : 4 * q + 4, :].bitcast(I32).rearrange("a r c -> r a c"))
+            by_row = wd_scales.bitcast(I32).rearrange("a (q r) c -> r q a c", r=4)
+            for r in range(4):
+                nc.sync.dma_start(out=wd_sc[r:P:32, :, :], in_=by_row[r])
 
         tab = [sb([P, T], I32, "tab%d" % a) for a in range(2)]
         w1_raw = {(a, b): sb([P, PACK, COLS], F32, "w1_raw%d%d" % (a, b)) for a in range(2) for b in range(2)}
@@ -100,7 +99,6 @@ def tile_list_meta_adapted_steps_kernel(tc, tab_words, tab_scales, offs, w1, b1,
         load_vectors()
         load_w1(0, 0)
         load_tab_scales()
-        load_wd_scales()
         load_tab(0)
         load_w1(1, 0)
 
@@ -219,15 +217,15 @@ def tile_list_meta_adapted_steps_kernel(tc, tab_words, tab_scales, offs, w1, b1,
                 nc.vector.tensor_scalar(out=res[:], in0=banks[s, n][:], scalar1=lr_sb[:, n, 0:1], scalar2=None, op0=MULT)
             nc.sync.dma_start(out=out[n * P : (n + 1) * P, s * COLS : (s + 1) * COLS], in_=res[:])
 
-        round_w1("scalar", 0, 0, VECTOR_SHARE_00, P)
-        round_w1("vector", 0, 0, 0, VECTOR_SHARE_00)
+        round_w1("scalar", 0, 0, 0, P)
         gather_scales()
         load_tab(1)
         move_scales()
         load_w1(0, 1)
         load_w1(1, 1)
-        load_wd()
         load_w2(0)
+        load_wd_scales()
+        load_wd()
         load_w2(1)
         load_lr()
         quantize("w1_00")
@@ -267,18 +265,18 @@ def tile_list_meta_adapted_steps_kernel(tc, tab_words, tab_scales, offs, w1, b1,
         quantize("h_00", MID, COLS, "b")
         quantize("w2_0")
         gain(1, 0)
-        round_w2("scalar", 1)
         gained_11a = gain_by_planes(1, 1, 0, MID, "a")
+        round_w2("scalar", 1)
         gained_11b = gain_by_planes(1, 1, MID, COLS, "b")
         interleave(0, 1, gained_01a, 0, MID)
         quantize("h_10")
-        quantize("w2_1")
-        quantize("h_01", 0, MID)
-        gain(0, 1, MID, COLS, "b")
         interleave(1, 1, gained_11a, 0, MID)
-        quantize("h_01", MID, COLS, "b")
+        quantize("h_01", 0, MID)
+        quantize("w2_1")
         quantize("h_11", 0, MID)
+        gain(0, 1, MID, COLS, "b")
         interleave(1, 1, gained_11b, MID, COLS)
+        quantize("h_01", MID, COLS, "b")
         quantize("h_11", MID, COLS)
 
         for n in range(OUT_TILES):
@@ -288,9 +286,11 @@ def tile_list_meta_adapted_steps_kernel(tc, tab_words, tab_scales, offs, w1, b1,
         for n in range(OUT_TILES):
             direct_passes(1, n)
         for n in range(OUT_TILES):
+            branch_pass(0, 1, n, 0, MID)
+        for n in range(OUT_TILES):
             branch_pass(1, 0, n)
             finish("scalar", 0, n)
-        for b, c0 in ((0, 0), (0, MID), (1, 0)):
+        for b, c0 in ((1, 0), (0, MID)):
             for n in range(OUT_TILES):
                 branch_pass(b, 1, n, c0, c0 + MID)
         for n in range(OUT_TILES):

@@ -1,6 +1,7 @@
 from contextlib import ExitStack
 
 import concourse.mybir as mybir
+from concourse.masks import make_identity
 
 K, T, S, H, N = 1024, 2048, 1024, 1024, 512
 FLOPS = 2 * S * (K * H + H * N + K * N)
@@ -53,15 +54,25 @@ def tile_list_meta_adapted_steps_kernel(tc, tab_words, tab_scales, offs, w1, b1,
         tab_sc = sb([P, T // 4], I32, "tab_sc")
         moved = sb([P, S // 4], I32, "moved")
         wd_sc = sb([P, 2, N // 4], I32, "wd_sc")
+        rows = sb([P, COLS], F32, "rows")
         nc.vector.memset(tab_sc[:], 0)
+        nc.vector.memset(rows[:], 0.0)
         nc.vector.memset(wd_sc[:], 0)
         nc.vector.memset(moved[:], 0)
-        per_r = sb([P, 4, 8], F32, "per_r")
+        ident = sb([P, P], F32, "ident")
+        make_identity(nc, ident[:])
+        per_r = sb([P, 4, PACK], F32, "per_r")
         lr_sb = sb([P, OUT_TILES, 8], F32, "lr_sb")
 
         def load_vectors():
-            nc.scalar.dma_start(out=per_r[:, 0:2, 0:PACK], in_=b1.rearrange("(b p t) -> p b t", b=2, t=PACK))
-            nc.scalar.dma_start(out=per_r[:, 2:4, 0:PACK], in_=g.rearrange("(b p t) -> p b t", b=2, t=PACK))
+            nc.scalar.dma_start(out=rows[0:2, :], in_=b1.rearrange("(b c) -> b c", b=2))
+            nc.scalar.dma_start(out=rows[2:4, :], in_=g.rearrange("(b c) -> b c", b=2))
+
+        def turn_vectors():
+            turned = psum.tile([P, PACK, P], F32, name="turned", tag="bank7")
+            for t in range(PACK):
+                nc.tensor.transpose(turned[:, t, :], rows[:, t:COLS:PACK], ident[:])
+            nc.scalar.activation(out=per_r[:], in_=turned[:, :, 0:4].rearrange("p t k -> p k t"), func=COPY)
 
         def load_lr():
             with nc.allow_non_contiguous_dma(reason="one rate for each partition and output tile"):
@@ -219,6 +230,7 @@ def tile_list_meta_adapted_steps_kernel(tc, tab_words, tab_scales, offs, w1, b1,
 
         round_w1("scalar", 0, 0, 0, P)
         gather_scales()
+        turn_vectors()
         load_tab(1)
         move_scales()
         load_w1(0, 1)

@@ -17,38 +17,46 @@ E5M2 = mybir.dt.float8_e5m2_x4
 TANH = mybir.ActivationFunctionType.Tanh
 COPY = mybir.ActivationFunctionType.Copy
 MULT = mybir.AluOpType.mult
+ADD = mybir.AluOpType.add
 
 P = 128
 PACK = 4
 PASS = P * PACK
 COLS = 512
 MID = COLS // 2
-QUADS = 4
 LOWER = 16
 GROUP = 16
 OUT_TILES = N // P
+ALIGN = 64
 
 VECTOR_SHARE_10 = 32
 
-SAME_BYTES = {
-    "rounded_h_00": "w1_raw01",
-    "rounded_h_00b": "w1_raw11",
-    "rounded_h_10": "w2_raw0",
-    "gained11b": "w2_raw1",
-    "rounded_h_01b": "rounded_w2_1",
-}
+GROUPS = {"h": (0, 0, COLS, (2, 3, 4, 5)), "q": (1, 0, MID, (6, 0, 1, 7)), "r": (1, MID, MID, (2, 3, 4, 5))}
+RING = 7
+GPSIMD_SHARE = 384
 
 
 def tile_list_meta_adapted_steps_kernel(tc, tab_words, tab_scales, offs, w1, b1, g, w2, wd_words, wd_scales, lr, out):
     nc = tc.nc
     with ExitStack() as ctx:
+        lists = ctx.enter_context(tc.tile_pool(name="lists", bufs=1))
         keep = ctx.enter_context(tc.tile_pool(name="keep", bufs=1))
         psum = ctx.enter_context(tc.psum_pool(name="psum", bufs=1))
 
-        def sb(shape, dtype, name):
-            return keep.tile(shape, dtype, name=name, tag=SAME_BYTES.get(name, name), align_bytes=64)
+        placed = {"end": 0}
 
-        offsets = keep.tile([P, S // GROUP], U16, name="offsets")
+        def sb(shape, dtype, name, on=None, at=0):
+            size = {F32: 4, I32: 4, U32: 4, BF16: 2, U8: 1}[dtype]
+            for d in shape[1:]:
+                size = size * d
+            if on is None:
+                placed[name] = placed["end"]
+                placed["end"] = placed["end"] + (size + ALIGN - 1) // ALIGN * ALIGN
+            else:
+                placed[name] = placed[on] + at
+            return keep.tile(shape, dtype, name=name, align_bytes=ALIGN, offset=placed[name])
+
+        offsets = lists.tile([P, S // GROUP], U16, name="offsets")
         nc.sync.dma_start(offsets[:], offs)
 
         tab_sc = sb([P, T // 4], I32, "tab_sc")
@@ -68,8 +76,9 @@ def tile_list_meta_adapted_steps_kernel(tc, tab_words, tab_scales, offs, w1, b1,
             nc.scalar.dma_start(out=rows[0:2, :], in_=b1.rearrange("(b c) -> b c", b=2))
             nc.scalar.dma_start(out=rows[2:4, :], in_=g.rearrange("(b c) -> b c", b=2))
 
+        turned = psum.tile([P, PACK, P], F32, name="turned", tag="bank7")
+
         def turn_vectors():
-            turned = psum.tile([P, PACK, P], F32, name="turned", tag="bank7")
             for t in range(PACK):
                 nc.tensor.transpose(turned[:, t, :], rows[:, t:COLS:PACK], ident[:])
             nc.scalar.activation(out=per_r[:], in_=turned[:, :, 0:4].rearrange("p t k -> p k t"), func=COPY)
@@ -107,18 +116,9 @@ def tile_list_meta_adapted_steps_kernel(tc, tab_words, tab_scales, offs, w1, b1,
         def load_wd():
             nc.sync.dma_start(out=wd[:], in_=wd_words.rearrange("a p c i -> p a (c i)").bitcast(I32))
 
-        load_vectors()
-        load_w1(0, 0)
-        load_tab_scales()
-        load_tab(0)
-        load_w1(1, 0)
-
-        v_codes, v_scales = {}, {}
-
         picked = sb([P, S // 4], I32, "picked")
-        for s in range(2):
-            v_scales[0, s] = picked[:].bitcast(U8)[:, s * COLS : (s + 1) * COLS]
-            v_scales[1, s] = moved[:].bitcast(U8)[:, s * COLS : (s + 1) * COLS]
+        v_scales = [picked, moved]
+        v_codes = {}
 
         def gather_scales():
             nc.vector.tensor_copy(picked[:].bitcast(U8), tab_sc[:].bitcast(U8).indirect(offsets[:]))
@@ -126,12 +126,14 @@ def tile_list_meta_adapted_steps_kernel(tc, tab_words, tab_scales, offs, w1, b1,
         def move_scales():
             nc.sync.dma_start(out=moved[0 : P - LOWER, :], in_=picked[LOWER:P, :])
 
-        def gather_words(a, s0, s1):
-            words = sb([P, (s1 - s0) * COLS], U32, "v_codes%d%d" % (a, s0))
-            entries = offsets[:, s0 * (COLS // GROUP) : s1 * (COLS // GROUP)]
-            nc.vector.tensor_copy(words[:], tab[a][:].bitcast(U32).indirect(entries))
-            for s in range(s0, s1):
-                v_codes[a, s] = words[:, (s - s0) * COLS : (s - s0 + 1) * COLS]
+        def gather_words(a, s):
+            v_codes[a, s] = sb([P, COLS], U32, "v_codes%d%d" % (a, s))
+            entries = offsets[:, s * (COLS // GROUP) : (s + 1) * (COLS // GROUP)]
+            nc.vector.tensor_copy(v_codes[a, s][:], tab[a][:].bitcast(U32).indirect(entries))
+
+        def table_operand(a, s, c0, width):
+            return (v_codes[a, s][:, c0 : c0 + width].bitcast(E5M2),
+                    v_scales[a][:].bitcast(U8)[:, s * COLS + c0 : s * COLS + c0 + width])
 
         def cast(engine, dst, src):
             if engine == "scalar":
@@ -141,93 +143,113 @@ def tile_list_meta_adapted_steps_kernel(tc, tab_words, tab_scales, offs, w1, b1,
 
         rounded, codes, scales = {}, {}, {}
 
-        def staged(key):
+        def staged(key, width, on=None, at=0):
             if key not in rounded:
-                rounded[key] = sb([P, PACK * COLS], BF16, "rounded_" + key)
+                rounded[key] = sb([P, PACK * width], BF16, "rounded_" + key, on, at)
             return rounded[key]
 
         def round_w1(engine, a, b, m0, m1):
             pairs = slice(m0 // 2, m1 // 2)
-            dst = staged("w1_%d%d" % (a, b))[:].rearrange("p (t m e j) -> p m j e t", t=PACK, e=2, j=PACK)
+            dst = staged("w1_%d%d" % (a, b), COLS)[:].rearrange("p (t m e j) -> p m j e t", t=PACK, e=2, j=PACK)
             src = w1_raw[a, b][:].rearrange("p j (m e t) -> p m j e t", e=2, t=PACK)
             cast(engine, dst[:, pairs, :, :, :], src[:, pairs, :, :, :])
 
-        def round_w2(engine, b):
-            dst = staged("w2_%d" % b)[:].rearrange("p (c e j) -> p c j e", e=2, j=PACK)
+        def round_w2(engine, b, c0=0, c1=COLS):
+            dst = staged("w2_%d" % b, COLS)[:].rearrange("p (c e j) -> p c j e", e=2, j=PACK)
             src = w2_raw[b][:].rearrange("p j (c e) -> p c j e", e=2)
-            cast(engine, dst, src)
+            pairs = slice(c0 // 2, c1 // 2)
+            cast(engine, dst[:, pairs], src[:, pairs])
 
-        def quantize(key, c0=0, c1=COLS, part=""):
+        def round_w2_gpsimd(b, c0, c1):
+            dst = staged("w2_%d" % b, COLS)[:].rearrange("p (c j) -> p c j", j=PACK)
+            src = w2_raw[b][:].rearrange("p j c -> p c j")
+            nc.gpsimd.tensor_scalar(out=dst[:, c0:c1], in0=src[:, c0:c1], scalar1=1.0, scalar2=0.0, op0=MULT, op1=ADD)
+
+        def quantize(key, c0, c1, width, source=None, on=None, at=0):
             if key not in codes:
-                codes[key] = sb([P, COLS], U32, "codes_" + key)
-                scales[key] = sb([P, COLS], U8, "scales_" + key)
-            nc.vector.quantize_mx(out=codes[key][:, c0:c1].bitcast(E4M3), scales=scales[key][:, c0:c1],
-                                  in_=rounded[key + part][:, PACK * c0 : PACK * c1])
+                codes[key] = sb([P, width], U32, "codes_" + key, on, at)
+                scales[key] = sb([P, width], U8, "scales_" + key)
+            values = rounded[key][:, PACK * c0 : PACK * c1] if source is None else rounded[source][:]
+            nc.vector.quantize_mx(out=codes[key][:, c0:c1].bitcast(E4M3), scales=scales[key][:, c0:c1], in_=values)
 
         banks = {}
 
-        def opened(s, i):
-            bk = 4 * s + i
-            banks[s, i] = psum.tile([P, COLS], F32, name="bank%d" % bk, tag="bank%d" % bk)
-            return banks[s, i]
+        def opened(bk):
+            banks[bk] = psum.tile([P, COLS], F32, name="bank%d" % bk, tag="bank%d" % bk)
+            return banks[bk]
 
         def hidden_pass(b, s, t, a):
-            acc = opened(s, t) if a == 0 else banks[s, t]
+            bk = (8 * b + 4 * s + t) % RING
+            acc = opened(bk) if a == 0 else banks[bk]
             key = "w1_%d%d" % (a, b)
             cols = slice(t * P, (t + 1) * P)
+            words, row_scales = table_operand(a, s, 0, COLS)
             nc.tensor.matmul_mx(out=acc[:], lhsT=codes[key][:, cols].bitcast(E4M3), lhsT_scale=scales[key][:, cols],
-                                rhs=v_codes[a, s].bitcast(E5M2), rhs_scale=v_scales[a, s],
-                                start=(a == 0), stop=(a == 1))
+                                rhs=words, rhs_scale=row_scales, start=(a == 0), stop=(a == 1))
 
         tanh_out = {}
 
         def tanh_plane(b, s, t):
             if (b, s) not in tanh_out:
                 tanh_out[b, s] = sb([P, PACK, COLS], F32, "tanh_out%d%d" % (b, s))
-            nc.scalar.activation(out=tanh_out[b, s][:, t, :], in_=banks[s, t][:], func=TANH, bias=per_r[:, b, t : t + 1])
+            nc.scalar.activation(out=tanh_out[b, s][:, t, :], in_=banks[(8 * b + 4 * s + t) % RING][:], func=TANH, bias=per_r[:, b, t : t + 1])
 
-        def gain(b, s, c0=0, c1=COLS, part=""):
-            pairs = slice(c0 // 2, c1 // 2)
-            dst = staged("h_%d%d" % (b, s) + part)[:].rearrange("p (c e t) -> p c t e", e=2, t=PACK)
-            src = tanh_out[b, s][:].rearrange("p t (c e) -> p c t e", e=2)
-            gains = per_r[:, 2 + b, 0:PACK].unsqueeze(1).unsqueeze(3).to_broadcast([P, (c1 - c0) // 2, PACK, 2])
-            nc.vector.tensor_tensor(out=dst[:, pairs, :, :], in0=src[:, pairs, :, :], in1=gains, op=MULT)
+        def gain(b, s, c0, c1, key, on=None, at=0, from_psum=False):
+            dst = staged(key, c1 - c0, on, at)[:].rearrange("p (c e t) -> p c t e", e=2, t=PACK)
+            src = tanh_out[b, s][:, :, c0:c1].rearrange("p t (c e) -> p c t e", e=2)
+            gains = turned[:, :, 2 + b] if from_psum else per_r[:, 2 + b, 0:PACK]
+            gains = gains.unsqueeze(1).unsqueeze(3).to_broadcast([P, (c1 - c0) // 2, PACK, 2])
+            nc.vector.tensor_tensor(out=dst, in0=src, in1=gains, op=MULT)
 
-        def gain_by_planes(b, s, c0, c1, part):
-            gained = sb([P, PACK, c1 - c0], BF16, "gained%d%d" % (b, s) + part)
+        def gain_by_planes(b, s, c0, c1, key, on=None, at=0):
+            gained = sb([P, PACK, c1 - c0], BF16, "gained_" + key, on, at)
             for t in range(PACK):
                 nc.scalar.activation(out=gained[:, t, :], in_=tanh_out[b, s][:, t, c0:c1], func=COPY,
                                      scale=per_r[:, 2 + b, t : t + 1])
             return gained
 
-        def interleave(b, s, gained, c0, c1):
-            dst = staged("h_%d%d" % (b, s))[:, PACK * c0 : PACK * c1].rearrange("p (c e t) -> p c t e", e=4, t=PACK)
+        def interleave(gained, key, width):
+            dst = staged(key, width)[:].rearrange("p (c e t) -> p c t e", e=4, t=PACK)
             nc.vector.tensor_copy(out=dst, in_=gained[:].rearrange("p t (c e) -> p c t e", e=4))
 
-        def direct_passes(s, n):
-            acc = opened(s, n)
+        def direct_passes(group, n):
+            s, c0, width, bank_of = GROUPS[group]
+            acc = opened(bank_of[n])
             cols = slice(n * P, (n + 1) * P)
             for a in range(2):
-                nc.tensor.matmul_mx(out=acc[:], lhsT=wd[:, a, cols].bitcast(E4M3),
+                words, row_scales = table_operand(a, s, c0, width)
+                nc.tensor.matmul_mx(out=acc[:, 0:width], lhsT=wd[:, a, cols].bitcast(E4M3),
                                     lhsT_scale=wd_sc[:, a, :].bitcast(U8)[:, cols],
-                                    rhs=v_codes[a, s].bitcast(E5M2), rhs_scale=v_scales[a, s],
-                                    start=(a == 0), stop=False)
+                                    rhs=words, rhs_scale=row_scales, start=(a == 0), stop=False)
 
-        def branch_pass(b, s, n, c0=0, c1=COLS):
+        def branch_pass(b, group, n):
+            s, c0, width, bank_of = GROUPS[group]
             cols = slice(n * P, (n + 1) * P)
-            wk, hk = "w2_%d" % b, "h_%d%d" % (b, s)
-            nc.tensor.matmul_mx(out=banks[s, n][:, c0:c1], lhsT=codes[wk][:, cols].bitcast(E4M3), lhsT_scale=scales[wk][:, cols],
-                                rhs=codes[hk][:, c0:c1].bitcast(E4M3), rhs_scale=scales[hk][:, c0:c1],
-                                start=False, stop=(b == 1 and c1 == COLS))
+            wk, hk = "w2_%d" % b, "h_%d%s" % (b, group)
+            nc.tensor.matmul_mx(out=banks[bank_of[n]][:, 0:width], lhsT=codes[wk][:, cols].bitcast(E4M3),
+                                lhsT_scale=scales[wk][:, cols], rhs=codes[hk][:].bitcast(E4M3), rhs_scale=scales[hk][:],
+                                start=False, stop=(b == 1))
 
-        def finish(engine, s, n):
-            res = sb([P, COLS], F32, "res%d%d_0" % (s, n))
-            if engine == "scalar":
-                nc.scalar.activation(out=res[:], in_=banks[s, n][:], func=COPY, scale=lr_sb[:, n, 0:1])
-            else:
-                nc.vector.tensor_scalar(out=res[:], in0=banks[s, n][:], scalar1=lr_sb[:, n, 0:1], scalar2=None, op0=MULT)
-            nc.sync.dma_start(out=out[n * P : (n + 1) * P, s * COLS : (s + 1) * COLS], in_=res[:])
+        out_tiles = out.rearrange("(n p) c -> p n c", p=P)
 
+        def finish(engine, group, n0, count):
+            s, c0, width, bank_of = GROUPS[group]
+            res = sb([P, count, width], F32, "res_%s%d" % (group, n0))
+            for i in range(count):
+                acc = banks[bank_of[n0 + i]][:, 0:width]
+                rate = lr_sb[:, n0 + i, 0:1]
+                if engine == "scalar":
+                    nc.scalar.activation(out=res[:, i, :], in_=acc, func=COPY, scale=rate)
+                else:
+                    nc.vector.tensor_scalar(out=res[:, i, :], in0=acc, scalar1=rate, scalar2=None, op0=MULT)
+            first_col = s * COLS + c0
+            nc.sync.dma_start(out=out_tiles[:, n0 : n0 + count, first_col : first_col + width], in_=res[:])
+
+        load_vectors()
+        load_w1(0, 0)
+        load_tab_scales()
+        load_tab(0)
+        load_w1(1, 0)
         round_w1("scalar", 0, 0, 0, P)
         gather_scales()
         turn_vectors()
@@ -240,71 +262,75 @@ def tile_list_meta_adapted_steps_kernel(tc, tab_words, tab_scales, offs, w1, b1,
         load_wd()
         load_w2(1)
         load_lr()
-        quantize("w1_00")
-        gather_words(0, 0, 1)
-        gather_words(0, 1, 2)
+        quantize("w1_00", 0, COLS, COLS)
+        gather_words(0, 0)
+        gather_words(0, 1)
         round_w1("scalar", 1, 0, VECTOR_SHARE_10, P)
         round_w1("vector", 1, 0, 0, VECTOR_SHARE_10)
-        quantize("w1_10")
-        gather_words(1, 0, 1)
-        gather_words(1, 1, 2)
+        quantize("w1_10", 0, COLS, COLS)
+        gather_words(1, 0)
+        gather_words(1, 1)
         round_w1("vector", 0, 1, 0, P)
-        quantize("w1_01")
+        quantize("w1_01", 0, COLS, COLS)
         round_w1("vector", 1, 1, 0, P)
-        quantize("w1_11", 0, MID)
-        quantize("w1_11", MID, COLS)
+        quantize("w1_11", 0, MID, COLS)
+        quantize("w1_11", MID, COLS, COLS)
 
-        for s in range(2):
-            for t in range(PACK):
-                hidden_pass(0, s, t, 0)
-        for s in range(2):
-            for t in range(PACK):
-                hidden_pass(0, s, t, 1)
-                tanh_plane(0, s, t)
-        for s in range(2):
-            for t in range(PACK):
-                hidden_pass(1, s, t, 0)
-        for s in range(2):
-            for t in range(PACK):
-                hidden_pass(1, s, t, 1)
-                tanh_plane(1, s, t)
+        planes = [(b, s, t) for b in range(2) for s in range(2) for t in range(PACK)]
+        for b, s, t in planes[:RING]:
+            hidden_pass(b, s, t, 0)
+        for u, (b, s, t) in enumerate(planes):
+            hidden_pass(b, s, t, 1)
+            tanh_plane(b, s, t)
+            if u + RING < len(planes):
+                hidden_pass(*planes[u + RING], 0)
 
-        gain(0, 0, 0, MID)
-        gain(0, 0, MID, COLS, "b")
-        gained_01a = gain_by_planes(0, 1, 0, MID, "a")
+        gain(0, 0, 0, MID, "h_0ha", on="w1_raw01")
+        gain(0, 0, MID, COLS, "h_0hb", on="w1_raw11")
+        gained_0q = gain_by_planes(0, 1, 0, MID, "0q")
         round_w2("vector", 0)
-        quantize("h_00", 0, MID)
-        quantize("h_00", MID, COLS, "b")
-        quantize("w2_0")
-        gain(1, 0)
-        gained_11a = gain_by_planes(1, 1, 0, MID, "a")
-        round_w2("scalar", 1)
-        gained_11b = gain_by_planes(1, 1, MID, COLS, "b")
-        interleave(0, 1, gained_01a, 0, MID)
-        quantize("h_10")
-        interleave(1, 1, gained_11a, 0, MID)
-        quantize("h_01", 0, MID)
-        quantize("w2_1")
-        quantize("h_11", 0, MID)
-        gain(0, 1, MID, COLS, "b")
-        interleave(1, 1, gained_11b, MID, COLS)
-        quantize("h_01", MID, COLS, "b")
-        quantize("h_11", MID, COLS)
+        quantize("h_0h", 0, MID, COLS, source="h_0ha")
+        quantize("h_0h", MID, COLS, COLS, source="h_0hb")
+        quantize("w2_0", 0, COLS, COLS)
+        gain(1, 0, 0, COLS, "h_1h", on="w2_raw0", from_psum=True)
+        staged("w2_1", COLS, on="rounded_w2_0")
+        round_w2_gpsimd(1, 0, GPSIMD_SHARE)
+        round_w2("scalar", 1, GPSIMD_SHARE, COLS)
+        gained_1q = gain_by_planes(1, 1, 0, MID, "1q", on="w2_raw1")
+        gained_1r = gain_by_planes(1, 1, MID, COLS, "1r", on="w2_raw1", at=2048)
+        quantize("h_1h", 0, COLS, COLS)
+        quantize("w2_1", 0, COLS, COLS)
+        staged("h_0q", MID, on="rounded_w2_1")
+        interleave(gained_0q, "h_0q", MID)
+        staged("h_1q", MID, on="rounded_w2_1", at=2048)
+        interleave(gained_1q, "h_1q", MID)
+        quantize("h_0q", 0, MID, MID)
+        quantize("h_1q", 0, MID, MID)
+        gain(0, 1, MID, COLS, "h_0r", on="rounded_h_0q")
+        staged("h_1r", MID, on="rounded_h_1q")
+        interleave(gained_1r, "h_1r", MID)
+        quantize("h_0r", 0, MID, MID)
+        quantize("h_1r", 0, MID, MID)
 
         for n in range(OUT_TILES):
-            direct_passes(0, n)
+            direct_passes("h", n)
         for n in range(OUT_TILES):
-            branch_pass(0, 0, n)
+            branch_pass(0, "h", n)
         for n in range(OUT_TILES):
-            direct_passes(1, n)
+            direct_passes("q", n)
         for n in range(OUT_TILES):
-            branch_pass(0, 1, n, 0, MID)
+            branch_pass(0, "q", n)
         for n in range(OUT_TILES):
-            branch_pass(1, 0, n)
-            finish("scalar", 0, n)
-        for b, c0 in ((1, 0), (0, MID)):
+            branch_pass(1, "h", n)
+            finish("scalar", "h", n, 1)
+        for n in range(OUT_TILES):
+            direct_passes("r", n)
+        for n in range(OUT_TILES):
+            branch_pass(1, "q", n)
+        finish("scalar", "q", 0, 2)
+        finish("scalar", "q", 2, 2)
+        for b in range(2):
             for n in range(OUT_TILES):
-                branch_pass(b, 1, n, c0, c0 + MID)
+                branch_pass(b, "r", n)
         for n in range(OUT_TILES):
-            branch_pass(1, 1, n, MID, COLS)
-            finish("vector" if n % 2 else "scalar", 1, n)
+            finish("scalar" if n % 2 else "vector", "r", n, 1)

@@ -33,7 +33,6 @@ VECTOR_SHARE_10 = 32
 
 GROUPS = {"h": (0, 0, COLS, (2, 3, 4, 5)), "q": (1, 0, MID, (6, 0, 1, 7)), "r": (1, MID, MID, (2, 3, 4, 5))}
 RING = 7
-GPSIMD_SHARE = 384
 
 
 def tile_list_meta_adapted_steps_kernel(tc, tab_words, tab_scales, offs, w1, b1, g, w2, wd_words, wd_scales, lr, out):
@@ -94,7 +93,9 @@ def tile_list_meta_adapted_steps_kernel(tc, tab_words, tab_scales, offs, w1, b1,
 
         tab = [sb([P, T], I32, "tab%d" % a) for a in range(2)]
         w1_raw = {(a, b): sb([P, PACK, COLS], F32, "w1_raw%d%d" % (a, b)) for a in range(2) for b in range(2)}
-        w2_raw = [sb([P, PACK, N], F32, "w2_raw%d" % b) for b in range(2)]
+        w2_raw = {(0, 0): sb([P, PACK, N], F32, "w2_raw0")}
+        for c0 in (0, MID):
+            w2_raw[1, c0] = sb([P, PACK, MID], F32, "w2_raw1_%d" % c0)
         wd = sb([P, 2, N], I32, "wd")
 
         def load_tab(a):
@@ -104,9 +105,9 @@ def tile_list_meta_adapted_steps_kernel(tc, tab_words, tab_scales, offs, w1, b1,
             part = w1[a * PASS : (a + 1) * PASS, b * COLS : (b + 1) * COLS]
             nc.sync.dma_start(out=w1_raw[a, b][:], in_=part.rearrange("(p j) c -> p j c", j=PACK))
 
-        def load_w2(b):
-            part = w2[b * PASS : (b + 1) * PASS, :]
-            nc.sync.dma_start(out=w2_raw[b][:], in_=part.rearrange("(p j) c -> p j c", j=PACK))
+        def load_w2(b, c0, c1):
+            part = w2[b * PASS : (b + 1) * PASS, c0:c1]
+            nc.sync.dma_start(out=w2_raw[b, c0][:], in_=part.rearrange("(p j) c -> p j c", j=PACK))
 
         def load_tab_scales():
             by_row = tab_scales.bitcast(I32).rearrange("a (q r) c -> r q a c", r=4)
@@ -154,16 +155,15 @@ def tile_list_meta_adapted_steps_kernel(tc, tab_words, tab_scales, offs, w1, b1,
             src = w1_raw[a, b][:].rearrange("p j (m e t) -> p m j e t", e=2, t=PACK)
             cast(engine, dst[:, pairs, :, :, :], src[:, pairs, :, :, :])
 
-        def round_w2(engine, b, c0=0, c1=COLS):
-            dst = staged("w2_%d" % b, COLS)[:].rearrange("p (c e j) -> p c j e", e=2, j=PACK)
-            src = w2_raw[b][:].rearrange("p j (c e) -> p c j e", e=2)
-            pairs = slice(c0 // 2, c1 // 2)
-            cast(engine, dst[:, pairs], src[:, pairs])
+        def round_w2(engine, b, c0, c1, first=0):
+            dst = staged("w2_%d" % b, COLS)[:, PACK * c0 : PACK * c1].rearrange("p (c e j) -> p c j e", e=2, j=PACK)
+            src = w2_raw[b, first][:, :, c0 - first : c1 - first].rearrange("p j (c e) -> p c j e", e=2)
+            cast(engine, dst, src)
 
-        def round_w2_gpsimd(b, c0, c1):
-            dst = staged("w2_%d" % b, COLS)[:].rearrange("p (c j) -> p c j", j=PACK)
-            src = w2_raw[b][:].rearrange("p j c -> p c j")
-            nc.gpsimd.tensor_scalar(out=dst[:, c0:c1], in0=src[:, c0:c1], scalar1=1.0, scalar2=0.0, op0=MULT, op1=ADD)
+        def round_w2_gpsimd(b, c0, c1, first=0):
+            dst = staged("w2_%d" % b, COLS)[:, PACK * c0 : PACK * c1].rearrange("p (c j) -> p c j", j=PACK)
+            src = w2_raw[b, first][:, :, c0 - first : c1 - first].rearrange("p j c -> p c j")
+            nc.gpsimd.tensor_scalar(out=dst, in0=src, scalar1=1.0, scalar2=0.0, op0=MULT, op1=ADD)
 
         def quantize(key, c0, c1, width, source=None, on=None, at=0):
             if key not in codes:
@@ -257,10 +257,11 @@ def tile_list_meta_adapted_steps_kernel(tc, tab_words, tab_scales, offs, w1, b1,
         move_scales()
         load_w1(0, 1)
         load_w1(1, 1)
-        load_w2(0)
+        load_w2(0, 0, N)
+        load_w2(1, 0, MID)
         load_wd_scales()
         load_wd()
-        load_w2(1)
+        load_w2(1, MID, N)
         load_lr()
         quantize("w1_00", 0, COLS, COLS)
         gather_words(0, 0)
@@ -288,27 +289,26 @@ def tile_list_meta_adapted_steps_kernel(tc, tab_words, tab_scales, offs, w1, b1,
         gain(0, 0, 0, MID, "h_0ha", on="w1_raw01")
         gain(0, 0, MID, COLS, "h_0hb", on="w1_raw11")
         gained_0q = gain_by_planes(0, 1, 0, MID, "0q")
-        round_w2("vector", 0)
+        round_w2("vector", 0, 0, COLS)
         quantize("h_0h", 0, MID, COLS, source="h_0ha")
         quantize("h_0h", MID, COLS, COLS, source="h_0hb")
         quantize("w2_0", 0, COLS, COLS)
         gain(1, 0, 0, COLS, "h_1h", on="w2_raw0", from_psum=True)
         staged("w2_1", COLS, on="rounded_w2_0")
-        round_w2_gpsimd(1, 0, GPSIMD_SHARE)
-        round_w2("scalar", 1, GPSIMD_SHARE, COLS)
-        gained_1q = gain_by_planes(1, 1, 0, MID, "1q", on="w2_raw1")
-        gained_1r = gain_by_planes(1, 1, MID, COLS, "1r", on="w2_raw1", at=2048)
+        round_w2_gpsimd(1, 0, MID)
+        round_w2("scalar", 1, MID, COLS, MID)
+        gained_1q = gain_by_planes(1, 1, 0, MID, "1q", on="w2_raw1_256")
+        quantize("w2_1", 0, MID, COLS)
         quantize("h_1h", 0, COLS, COLS)
-        quantize("w2_1", 0, COLS, COLS)
+        quantize("w2_1", MID, COLS, COLS)
         staged("h_0q", MID, on="rounded_w2_1")
-        interleave(gained_0q, "h_0q", MID)
         staged("h_1q", MID, on="rounded_w2_1", at=2048)
+        interleave(gained_0q, "h_0q", MID)
         interleave(gained_1q, "h_1q", MID)
         quantize("h_0q", 0, MID, MID)
         quantize("h_1q", 0, MID, MID)
         gain(0, 1, MID, COLS, "h_0r", on="rounded_h_0q")
-        staged("h_1r", MID, on="rounded_h_1q")
-        interleave(gained_1r, "h_1r", MID)
+        gain(1, 1, MID, COLS, "h_1r", on="rounded_h_1q")
         quantize("h_0r", 0, MID, MID)
         quantize("h_1r", 0, MID, MID)
 
@@ -319,10 +319,10 @@ def tile_list_meta_adapted_steps_kernel(tc, tab_words, tab_scales, offs, w1, b1,
         for n in range(OUT_TILES):
             direct_passes("q", n)
         for n in range(OUT_TILES):
-            branch_pass(0, "q", n)
-        for n in range(OUT_TILES):
             branch_pass(1, "h", n)
             finish("scalar", "h", n, 1)
+        for n in range(OUT_TILES):
+            branch_pass(0, "q", n)
         for n in range(OUT_TILES):
             direct_passes("r", n)
         for n in range(OUT_TILES):

@@ -31,8 +31,9 @@ ALIGN = 64
 
 VECTOR_SHARE_10 = 32
 
-GROUPS = {"h": (0, 0, COLS, (2, 3, 4, 5)), "q": (1, 0, MID, (6, 0, 1, 7)), "r": (1, MID, MID, (2, 3, 4, 5))}
+GROUPS = {"h": (0, 0, COLS, (2, 3, 4, 5)), "q": (1, 0, MID, (6, 6, 0, 0)), "r": (1, MID, MID, (1, 7, 2, 3))}
 RING = 7
+GPSIMD_SHARE = 256
 
 
 def tile_list_meta_adapted_steps_kernel(tc, tab_words, tab_scales, offs, w1, b1, g, w2, wd_words, wd_scales, lr, out):
@@ -212,31 +213,39 @@ def tile_list_meta_adapted_steps_kernel(tc, tab_words, tab_scales, offs, w1, b1,
             dst = staged(key, width)[:].rearrange("p (c e t) -> p c t e", e=4, t=PACK)
             nc.vector.tensor_copy(out=dst, in_=gained[:].rearrange("p t (c e) -> p c t e", e=4))
 
+        def sum_of(group, n):
+            s, c0, width, bank_of = GROUPS[group]
+            bk = bank_of[n]
+            place = bank_of[:n].count(bk)
+            return bk, slice(place * width, (place + 1) * width), place == 0, place == bank_of.count(bk) - 1
+
         def direct_passes(group, n):
             s, c0, width, bank_of = GROUPS[group]
-            acc = opened(bank_of[n])
+            bk, where, first, last = sum_of(group, n)
+            acc = opened(bk) if first else banks[bk]
             cols = slice(n * P, (n + 1) * P)
             for a in range(2):
                 words, row_scales = table_operand(a, s, c0, width)
-                nc.tensor.matmul_mx(out=acc[:, 0:width], lhsT=wd[:, a, cols].bitcast(E4M3),
+                nc.tensor.matmul_mx(out=acc[:, where], lhsT=wd[:, a, cols].bitcast(E4M3),
                                     lhsT_scale=wd_sc[:, a, :].bitcast(U8)[:, cols],
-                                    rhs=words, rhs_scale=row_scales, start=(a == 0), stop=False)
+                                    rhs=words, rhs_scale=row_scales, start=(first and a == 0), stop=False)
 
         def branch_pass(b, group, n):
-            s, c0, width, bank_of = GROUPS[group]
+            bk, where, first, last = sum_of(group, n)
             cols = slice(n * P, (n + 1) * P)
             wk, hk = "w2_%d" % b, "h_%d%s" % (b, group)
-            nc.tensor.matmul_mx(out=banks[bank_of[n]][:, 0:width], lhsT=codes[wk][:, cols].bitcast(E4M3),
+            nc.tensor.matmul_mx(out=banks[bk][:, where], lhsT=codes[wk][:, cols].bitcast(E4M3),
                                 lhsT_scale=scales[wk][:, cols], rhs=codes[hk][:].bitcast(E4M3), rhs_scale=scales[hk][:],
-                                start=False, stop=(b == 1))
+                                start=False, stop=(last and b == 1))
 
         out_tiles = out.rearrange("(n p) c -> p n c", p=P)
 
-        def finish(engine, group, n0, count):
+        def finish(engine, group, n0, count, on=None):
             s, c0, width, bank_of = GROUPS[group]
-            res = sb([P, count, width], F32, "res_%s%d" % (group, n0))
+            res = sb([P, count, width], F32, "res_%s%d" % (group, n0), on)
             for i in range(count):
-                acc = banks[bank_of[n0 + i]][:, 0:width]
+                bk, where, first, last = sum_of(group, n0 + i)
+                acc = banks[bk][:, where]
                 rate = lr_sb[:, n0 + i, 0:1]
                 if engine == "scalar":
                     nc.scalar.activation(out=res[:, i, :], in_=acc, func=COPY, scale=rate)
@@ -287,29 +296,30 @@ def tile_list_meta_adapted_steps_kernel(tc, tab_words, tab_scales, offs, w1, b1,
                 hidden_pass(*planes[u + RING], 0)
 
         gain(0, 0, 0, MID, "h_0ha", on="w1_raw01")
-        gain(0, 0, MID, COLS, "h_0hb", on="w1_raw11")
+        gain(0, 0, MID, COLS, "h_0hb", on="w1_raw11", from_psum=True)
+        gain(0, 1, MID, COLS, "h_0r", on="w1_raw11", at=2048, from_psum=True)
         gained_0q = gain_by_planes(0, 1, 0, MID, "0q")
-        round_w2("vector", 0, 0, COLS)
+        staged("w2_0", COLS, on="rounded_w1_11")
+        round_w2_gpsimd(0, 0, GPSIMD_SHARE)
+        round_w2("vector", 0, GPSIMD_SHARE, COLS)
         quantize("h_0h", 0, MID, COLS, source="h_0ha")
         quantize("h_0h", MID, COLS, COLS, source="h_0hb")
         quantize("w2_0", 0, COLS, COLS)
         gain(1, 0, 0, COLS, "h_1h", on="w2_raw0", from_psum=True)
         staged("w2_1", COLS, on="rounded_w2_0")
         round_w2_gpsimd(1, 0, MID)
+        gained_1q = gain_by_planes(1, 1, 0, MID, "1q")
         round_w2("scalar", 1, MID, COLS, MID)
-        gained_1q = gain_by_planes(1, 1, 0, MID, "1q", on="w2_raw1_256")
         quantize("w2_1", 0, MID, COLS)
         quantize("h_1h", 0, COLS, COLS)
-        quantize("w2_1", MID, COLS, COLS)
-        staged("h_0q", MID, on="rounded_w2_1")
-        staged("h_1q", MID, on="rounded_w2_1", at=2048)
+        staged("h_0q", MID, on="w2_raw0", at=4096)
         interleave(gained_0q, "h_0q", MID)
         interleave(gained_1q, "h_1q", MID)
-        quantize("h_0q", 0, MID, MID)
-        quantize("h_1q", 0, MID, MID)
-        gain(0, 1, MID, COLS, "h_0r", on="rounded_h_0q")
-        gain(1, 1, MID, COLS, "h_1r", on="rounded_h_1q")
-        quantize("h_0r", 0, MID, MID)
+        quantize("w2_1", MID, COLS, COLS)
+        quantize("h_0q", 0, MID, MID, on="rounded_w2_1")
+        quantize("h_1q", 0, MID, MID, on="rounded_w2_1", at=1024)
+        gain(1, 1, MID, COLS, "h_1r", on="rounded_h_0q")
+        quantize("h_0r", 0, MID, MID, on="rounded_h_1q")
         quantize("h_1r", 0, MID, MID)
 
         for n in range(OUT_TILES):
@@ -318,17 +328,20 @@ def tile_list_meta_adapted_steps_kernel(tc, tab_words, tab_scales, offs, w1, b1,
             branch_pass(0, "h", n)
         for n in range(OUT_TILES):
             direct_passes("q", n)
-        for n in range(OUT_TILES):
-            branch_pass(1, "h", n)
-            finish("scalar", "h", n, 1)
-        for n in range(OUT_TILES):
-            branch_pass(0, "q", n)
-        for n in range(OUT_TILES):
-            direct_passes("r", n)
-        for n in range(OUT_TILES):
-            branch_pass(1, "q", n)
+        for n0 in (0, 2):
+            for n in range(n0, n0 + 2):
+                branch_pass(1, "h", n)
+                finish("scalar", "h", n, 1, on="w2_raw1_256" if n == 0 else None)
+            if n0 == 0:
+                direct_passes("r", 0)
+                direct_passes("r", 1)
+        for b in range(2):
+            for n in range(OUT_TILES):
+                branch_pass(b, "q", n)
         finish("scalar", "q", 0, 2)
         finish("scalar", "q", 2, 2)
+        direct_passes("r", 2)
+        direct_passes("r", 3)
         for b in range(2):
             for n in range(OUT_TILES):
                 branch_pass(b, "r", n)

@@ -240,9 +240,9 @@ def tile_list_meta_adapted_steps_kernel(tc, tab_words, tab_scales, offs, w1, b1,
 
         out_tiles = out.rearrange("(n p) c -> p n c", p=P)
 
-        def finish(engine, group, n0, count, on=None):
+        def finish(engine, group, n0, count):
             s, c0, width, bank_of = GROUPS[group]
-            res = sb([P, count, width], F32, "res_%s%d" % (group, n0), on)
+            res = sb([P, count, width], F32, "res_%s%d" % (group, n0))
             for i in range(count):
                 bk, where, first, last = sum_of(group, n0 + i)
                 acc = banks[bk][:, where]
@@ -267,9 +267,9 @@ def tile_list_meta_adapted_steps_kernel(tc, tab_words, tab_scales, offs, w1, b1,
         load_w1(0, 1)
         load_w1(1, 1)
         load_w2(0, 0, N)
-        load_w2(1, 0, MID)
         load_wd_scales()
         load_wd()
+        load_w2(1, 0, MID)
         load_w2(1, MID, N)
         load_lr()
         quantize("w1_00", 0, COLS, COLS)
@@ -311,13 +311,14 @@ def tile_list_meta_adapted_steps_kernel(tc, tab_words, tab_scales, offs, w1, b1,
         gained_1q = gain_by_planes(1, 1, 0, MID, "1q")
         round_w2("scalar", 1, MID, COLS, MID)
         quantize("w2_1", 0, MID, COLS)
-        quantize("h_1h", 0, COLS, COLS)
-        staged("h_0q", MID, on="w2_raw0", at=4096)
+        quantize("h_1h", 0, COLS, COLS, on="w2_raw1_0")
+        staged("h_0q", MID, on="w2_raw1_0", at=2048)
         interleave(gained_0q, "h_0q", MID)
+        staged("h_1q", MID, on="rounded_h_1h")
         interleave(gained_1q, "h_1q", MID)
         quantize("w2_1", MID, COLS, COLS)
-        quantize("h_0q", 0, MID, MID, on="rounded_w2_1")
-        quantize("h_1q", 0, MID, MID, on="rounded_w2_1", at=1024)
+        quantize("h_0q", 0, MID, MID, on="w2_raw1_256")
+        quantize("h_1q", 0, MID, MID, on="w2_raw1_256", at=1024)
         gain(1, 1, MID, COLS, "h_1r", on="rounded_h_0q")
         quantize("h_0r", 0, MID, MID, on="rounded_h_1q")
         quantize("h_1r", 0, MID, MID)
@@ -331,7 +332,7 @@ def tile_list_meta_adapted_steps_kernel(tc, tab_words, tab_scales, offs, w1, b1,
         for n0 in (0, 2):
             for n in range(n0, n0 + 2):
                 branch_pass(1, "h", n)
-                finish("scalar", "h", n, 1, on="w2_raw1_256" if n == 0 else None)
+                finish("scalar", "h", n, 1)
             if n0 == 0:
                 direct_passes("r", 0)
                 direct_passes("r", 1)

@@ -33,7 +33,8 @@ VECTOR_SHARE_10 = 32
 
 GROUPS = {"h": (0, 0, COLS, (2, 3, 4, 5)), "q": (1, 0, MID, (6, 6, 0, 0)), "r": (1, MID, MID, (1, 7, 2, 3))}
 RING = 7
-GPSIMD_SHARE = 256
+GPSIMD_SHARE = 320
+EARLY = 128
 
 
 def tile_list_meta_adapted_steps_kernel(tc, tab_words, tab_scales, offs, w1, b1, g, w2, wd_words, wd_scales, lr, out):
@@ -295,15 +296,15 @@ def tile_list_meta_adapted_steps_kernel(tc, tab_words, tab_scales, offs, w1, b1,
             if u + RING < len(planes):
                 hidden_pass(*planes[u + RING], 0)
 
-        gain(0, 0, 0, MID, "h_0ha", on="w1_raw01")
-        gain(0, 0, MID, COLS, "h_0hb", on="w1_raw11", from_psum=True)
-        gain(0, 1, MID, COLS, "h_0r", on="w1_raw11", at=2048, from_psum=True)
+        gain(0, 0, 0, EARLY, "h_0ha", on="w1_raw01")
+        gain(0, 0, EARLY, COLS, "h_0hb", on="w1_raw11", from_psum=True)
+        gain(0, 1, MID, COLS, "h_0r", on="w1_raw11", at=4096, from_psum=True)
         gained_0q = gain_by_planes(0, 1, 0, MID, "0q")
         staged("w2_0", COLS, on="rounded_w1_11")
         round_w2_gpsimd(0, 0, GPSIMD_SHARE)
         round_w2("vector", 0, GPSIMD_SHARE, COLS)
-        quantize("h_0h", 0, MID, COLS, source="h_0ha")
-        quantize("h_0h", MID, COLS, COLS, source="h_0hb")
+        quantize("h_0h", 0, EARLY, COLS, source="h_0ha")
+        quantize("h_0h", EARLY, COLS, COLS, source="h_0hb")
         quantize("w2_0", 0, COLS, COLS)
         gain(1, 0, 0, COLS, "h_1h", on="w2_raw0", from_psum=True)
         staged("w2_1", COLS, on="rounded_w2_0")

@@ -32,8 +32,9 @@ ALIGN = 64
 VECTOR_SHARE_10 = 32
 
 GROUPS = {"h": (0, 0, COLS, (2, 3, 4, 5)), "q": (1, 0, MID, (6, 6, 0, 0)), "r": (1, MID, MID, (1, 7, 2, 3))}
+CLOSING = {"h": 1, "q": 0, "r": 0}
 RING = 7
-GPSIMD_SHARE = 320
+GPSIMD_SHARE = 160
 EARLY = 128
 
 
@@ -162,8 +163,9 @@ def tile_list_meta_adapted_steps_kernel(tc, tab_words, tab_scales, offs, w1, b1,
             src = w2_raw[b, first][:, :, c0 - first : c1 - first].rearrange("p j (c e) -> p c j e", e=2)
             cast(engine, dst, src)
 
-        def round_w2_gpsimd(b, c0, c1, first=0):
-            dst = staged("w2_%d" % b, COLS)[:, PACK * c0 : PACK * c1].rearrange("p (c j) -> p c j", j=PACK)
+        def round_w2_gpsimd(b, c0, c1, first=0, key=None):
+            dst = rounded[key][:] if key else staged("w2_%d" % b, COLS)[:, PACK * c0 : PACK * c1]
+            dst = dst.rearrange("p (c j) -> p c j", j=PACK)
             src = w2_raw[b, first][:, :, c0 - first : c1 - first].rearrange("p j c -> p c j")
             nc.gpsimd.tensor_scalar(out=dst, in0=src, scalar1=1.0, scalar2=0.0, op0=MULT, op1=ADD)
 
@@ -231,13 +233,16 @@ def tile_list_meta_adapted_steps_kernel(tc, tab_words, tab_scales, offs, w1, b1,
                                     lhsT_scale=wd_sc[:, a, :].bitcast(U8)[:, cols],
                                     rhs=words, rhs_scale=row_scales, start=(first and a == 0), stop=False)
 
-        def branch_pass(b, group, n):
+        def branch_pass(b, group, n, c0=0, c1=None):
             bk, where, first, last = sum_of(group, n)
             cols = slice(n * P, (n + 1) * P)
             wk, hk = "w2_%d" % b, "h_%d%s" % (b, group)
-            nc.tensor.matmul_mx(out=banks[bk][:, where], lhsT=codes[wk][:, cols].bitcast(E4M3),
-                                lhsT_scale=scales[wk][:, cols], rhs=codes[hk][:].bitcast(E4M3), rhs_scale=scales[hk][:],
-                                start=False, stop=(last and b == 1))
+            width = GROUPS[group][2]
+            c1 = width if c1 is None else c1
+            nc.tensor.matmul_mx(out=banks[bk][:, where][:, c0:c1], lhsT=codes[wk][:, cols].bitcast(E4M3),
+                                lhsT_scale=scales[wk][:, cols], rhs=codes[hk][:, c0:c1].bitcast(E4M3),
+                                rhs_scale=scales[hk][:, c0:c1], start=False,
+                                stop=(last and b == CLOSING[group] and c1 == width))
 
         out_tiles = out.rearrange("(n p) c -> p n c", p=P)
 
@@ -298,7 +303,6 @@ def tile_list_meta_adapted_steps_kernel(tc, tab_words, tab_scales, offs, w1, b1,
 
         gain(0, 0, 0, EARLY, "h_0ha", on="w1_raw01")
         gain(0, 0, EARLY, COLS, "h_0hb", on="w1_raw11", from_psum=True)
-        gain(0, 1, MID, COLS, "h_0r", on="w1_raw11", at=4096, from_psum=True)
         gained_0q = gain_by_planes(0, 1, 0, MID, "0q")
         staged("w2_0", COLS, on="rounded_w1_11")
         round_w2_gpsimd(0, 0, GPSIMD_SHARE)
@@ -309,43 +313,51 @@ def tile_list_meta_adapted_steps_kernel(tc, tab_words, tab_scales, offs, w1, b1,
         gain(1, 0, 0, COLS, "h_1h", on="w2_raw0", from_psum=True)
         staged("w2_1", COLS, on="rounded_w2_0")
         round_w2_gpsimd(1, 0, MID)
-        gained_1q = gain_by_planes(1, 1, 0, MID, "1q")
-        round_w2("scalar", 1, MID, COLS, MID)
+        round_w2("scalar", 1, 3 * P, COLS, MID)
+        gained_1r = gain_by_planes(1, 1, MID, COLS, "1r")
         quantize("w2_1", 0, MID, COLS)
         quantize("h_1h", 0, COLS, COLS, on="w2_raw1_0")
-        staged("h_0q", MID, on="w2_raw1_0", at=2048)
+        gain(1, 1, 0, MID, "h_1q", on="w2_raw1_0", at=2048, from_psum=True)
+        staged("w2_1c", P, on="rounded_h_1h")
+        round_w2_gpsimd(1, 2 * P, 3 * P, MID, key="w2_1c")
+        quantize("w2_1", 3 * P, COLS, COLS)
+        quantize("w2_1", 2 * P, 3 * P, COLS, source="w2_1c")
+        staged("h_0q", MID, on="rounded_h_1h", at=2048)
         interleave(gained_0q, "h_0q", MID)
-        staged("h_1q", MID, on="rounded_h_1h")
-        interleave(gained_1q, "h_1q", MID)
-        quantize("w2_1", MID, COLS, COLS)
-        quantize("h_0q", 0, MID, MID, on="w2_raw1_256")
-        quantize("h_1q", 0, MID, MID, on="w2_raw1_256", at=1024)
-        gain(1, 1, MID, COLS, "h_1r", on="rounded_h_0q")
-        quantize("h_0r", 0, MID, MID, on="rounded_h_1q")
+        quantize("h_1q", 0, MID, MID)
+        quantize("h_0q", 0, MID, MID)
+        staged("h_1r", MID, on="gained_0q")
+        interleave(gained_1r, "h_1r", MID)
+        gain(0, 1, MID, MID + P, "h_0r0", on="rounded_h_1q")
         quantize("h_1r", 0, MID, MID)
+        gain(0, 1, MID + P, COLS, "h_0r128", on="rounded_h_1q", at=1024)
+        for c0 in (0, P):
+            quantize("h_0r", c0, c0 + P, MID, source="h_0r%d" % c0)
 
         for n in range(OUT_TILES):
             direct_passes("h", n)
         for n in range(OUT_TILES):
             branch_pass(0, "h", n)
-        for n in range(OUT_TILES):
-            direct_passes("q", n)
         for n0 in (0, 2):
+            for n in range(n0, n0 + 2):
+                direct_passes("q", n)
+            if n0 == 2:
+                direct_passes("r", 0)
             for n in range(n0, n0 + 2):
                 branch_pass(1, "h", n)
                 finish("scalar", "h", n, 1)
-            if n0 == 0:
-                direct_passes("r", 0)
-                direct_passes("r", 1)
-        for b in range(2):
+        direct_passes("r", 1)
+        for b in (1, 0):
             for n in range(OUT_TILES):
                 branch_pass(b, "q", n)
         finish("scalar", "q", 0, 2)
         finish("scalar", "q", 2, 2)
-        direct_passes("r", 2)
-        direct_passes("r", 3)
-        for b in range(2):
+        for n in range(2, OUT_TILES):
+            direct_passes("r", n)
+        for n in range(OUT_TILES):
+            branch_pass(1, "r", n)
+        for c0 in (0, P):
             for n in range(OUT_TILES):
-                branch_pass(b, "r", n)
+                branch_pass(0, "r", n, c0, c0 + P)
         for n in range(OUT_TILES):
             finish("scalar" if n % 2 else "vector", "r", n, 1)

@@ -99,7 +99,7 @@ def tile_list_meta_adapted_steps_kernel(tc, tab_words, tab_scales, offs, w1, b1,
         w2_raw = {(0, 0): sb([P, PACK, N], F32, "w2_raw0")}
         for c0 in (0, MID):
             w2_raw[1, c0] = sb([P, PACK, MID], F32, "w2_raw1_%d" % c0)
-        wd = sb([P, 2, N], I32, "wd")
+        wd = [sb([P, N], I32, "wd%d" % a) for a in range(2)]
 
         def load_tab(a):
             nc.sync.dma_start(out=tab[a][:], in_=tab_words[a].rearrange("p c i -> p (c i)").bitcast(I32))
@@ -117,8 +117,8 @@ def tile_list_meta_adapted_steps_kernel(tc, tab_words, tab_scales, offs, w1, b1,
             for r in range(4):
                 nc.sync.dma_start(out=tab_sc[r:P:LOWER, :], in_=by_row[r])
 
-        def load_wd():
-            nc.sync.dma_start(out=wd[:], in_=wd_words.rearrange("a p c i -> p a (c i)").bitcast(I32))
+        def load_wd(a):
+            nc.sync.dma_start(out=wd[a][:], in_=wd_words[a].rearrange("p c i -> p (c i)").bitcast(I32))
 
         picked = sb([P, S // 4], I32, "picked")
         v_scales = [picked, moved]
@@ -222,16 +222,17 @@ def tile_list_meta_adapted_steps_kernel(tc, tab_words, tab_scales, offs, w1, b1,
             place = bank_of[:n].count(bk)
             return bk, slice(place * width, (place + 1) * width), place == 0, place == bank_of.count(bk) - 1
 
-        def direct_passes(group, n):
+        def direct_passes(group, n, passes=(1, 0), opens=True):
             s, c0, width, bank_of = GROUPS[group]
             bk, where, first, last = sum_of(group, n)
-            acc = opened(bk) if first else banks[bk]
             cols = slice(n * P, (n + 1) * P)
-            for a in range(2):
+            for a in passes:
+                start = first and opens and a == passes[0]
+                acc = opened(bk) if start else banks[bk]
                 words, row_scales = table_operand(a, s, c0, width)
-                nc.tensor.matmul_mx(out=acc[:, where], lhsT=wd[:, a, cols].bitcast(E4M3),
+                nc.tensor.matmul_mx(out=acc[:, where], lhsT=wd[a][:, cols].bitcast(E4M3),
                                     lhsT_scale=wd_sc[:, a, :].bitcast(U8)[:, cols],
-                                    rhs=words, rhs_scale=row_scales, start=(first and a == 0), stop=False)
+                                    rhs=words, rhs_scale=row_scales, start=start, stop=False)
 
         def branch_pass(b, group, n, c0=0, c1=None):
             bk, where, first, last = sum_of(group, n)
@@ -274,8 +275,9 @@ def tile_list_meta_adapted_steps_kernel(tc, tab_words, tab_scales, offs, w1, b1,
         load_w1(1, 1)
         load_w2(0, 0, N)
         load_wd_scales()
-        load_wd()
+        load_wd(0)
         load_w2(1, 0, MID)
+        load_wd(1)
         load_w2(1, MID, N)
         load_lr()
         quantize("w1_00", 0, COLS, COLS)
@@ -334,8 +336,10 @@ def tile_list_meta_adapted_steps_kernel(tc, tab_words, tab_scales, offs, w1, b1,
         for c0 in (0, P):
             quantize("h_0r", c0, c0 + P, MID, source="h_0r%d" % c0)
 
-        for n in range(OUT_TILES):
-            direct_passes("h", n)
+        for a in range(2):
+            for n in range(OUT_TILES - 1):
+                direct_passes("h", n, (a,), opens=(a == 0))
+        direct_passes("h", OUT_TILES - 1)
         for n in range(OUT_TILES):
             branch_pass(0, "h", n)
         for n0 in (0, 2):

@@ -342,22 +342,20 @@ def tile_list_meta_adapted_steps_kernel(tc, tab_words, tab_scales, offs, w1, b1,
         direct_passes("h", OUT_TILES - 1)
         for n in range(OUT_TILES):
             branch_pass(0, "h", n)
+        for n in range(OUT_TILES):
+            direct_passes("q", n)
         for n0 in (0, 2):
-            for n in range(n0, n0 + 2):
-                direct_passes("q", n)
-            if n0 == 2:
-                direct_passes("r", 0)
             for n in range(n0, n0 + 2):
                 branch_pass(1, "h", n)
                 finish("scalar", "h", n, 1)
-        direct_passes("r", 1)
+            for n in ((0, 1) if n0 == 0 else (2,)):
+                direct_passes("r", n)
         for b in (1, 0):
             for n in range(OUT_TILES):
                 branch_pass(b, "q", n)
         finish("scalar", "q", 0, 2)
         finish("scalar", "q", 2, 2)
-        for n in range(2, OUT_TILES):
-            direct_passes("r", n)
+        direct_passes("r", 3)
         for n in range(OUT_TILES):
             branch_pass(1, "r", n)
         for c0 in (0, P):

from contextlib import ExitStack

import concourse.mybir as mybir
from concourse.masks import make_identity

K, T, S, H, N = 1024, 2048, 1024, 1024, 512
FLOPS = 2 * S * (K * H + H * N + K * N)

F32 = mybir.dt.float32
BF16 = mybir.dt.bfloat16
I32 = mybir.dt.int32
U32 = mybir.dt.uint32
U16 = mybir.dt.uint16
U8 = mybir.dt.uint8
E4M3 = mybir.dt.float8_e4m3fn_x4
E5M2 = mybir.dt.float8_e5m2_x4
TANH = mybir.ActivationFunctionType.Tanh
COPY = mybir.ActivationFunctionType.Copy
MULT = mybir.AluOpType.mult
ADD = mybir.AluOpType.add

P = 128
PACK = 4
PASS = P * PACK
COLS = 512
MID = COLS // 2
LOWER = 16
GROUP = 16
OUT_TILES = N // P
ALIGN = 64

VECTOR_SHARE_10 = 32

GROUPS = {"h": (0, 0, COLS, (2, 3, 4, 5)), "q": (1, 0, MID, (6, 6, 0, 0)), "r": (1, MID, MID, (1, 7, 2, 3))}
CLOSING = {"h": 1, "q": 0, "r": 0}
RING = 7
GPSIMD_SHARE = 160
EARLY = 128


def tile_list_meta_adapted_steps_kernel(tc, tab_words, tab_scales, offs, w1, b1, g, w2, wd_words, wd_scales, lr, out):
    nc = tc.nc
    with ExitStack() as ctx:
        lists = ctx.enter_context(tc.tile_pool(name="lists", bufs=1))
        keep = ctx.enter_context(tc.tile_pool(name="keep", bufs=1))
        psum = ctx.enter_context(tc.psum_pool(name="psum", bufs=1))

        placed = {"end": 0}

        def sb(shape, dtype, name, on=None, at=0):
            size = {F32: 4, I32: 4, U32: 4, BF16: 2, U8: 1}[dtype]
            for d in shape[1:]:
                size = size * d
            if on is None:
                placed[name] = placed["end"]
                placed["end"] = placed["end"] + (size + ALIGN - 1) // ALIGN * ALIGN
            else:
                placed[name] = placed[on] + at
            return keep.tile(shape, dtype, name=name, align_bytes=ALIGN, offset=placed[name])

        offsets = lists.tile([P, S // GROUP], U16, name="offsets")
        nc.sync.dma_start(offsets[:], offs)

        tab_sc = sb([P, T // 4], I32, "tab_sc")
        moved = sb([P, S // 4], I32, "moved")
        wd_sc = sb([P, 2, N // 4], I32, "wd_sc")
        rows = sb([P, COLS], F32, "rows")
        nc.vector.memset(tab_sc[:], 0)
        nc.vector.memset(rows[:], 0.0)
        nc.vector.memset(wd_sc[:], 0)
        nc.vector.memset(moved[:], 0)
        ident = sb([P, P], F32, "ident")
        make_identity(nc, ident[:])
        per_r = sb([P, 4, PACK], F32, "per_r")
        lr_sb = sb([P, OUT_TILES, 8], F32, "lr_sb")

        def load_vectors():
            nc.scalar.dma_start(out=rows[0:2, :], in_=b1.rearrange("(b c) -> b c", b=2))
            nc.scalar.dma_start(out=rows[2:4, :], in_=g.rearrange("(b c) -> b c", b=2))

        turned = psum.tile([P, PACK, P], F32, name="turned", tag="bank7")

        def turn_vectors():
            for t in range(PACK):
                nc.tensor.transpose(turned[:, t, :], rows[:, t:COLS:PACK], ident[:])
            nc.scalar.activation(out=per_r[:], in_=turned[:, :, 0:4].rearrange("p t k -> p k t"), func=COPY)

        def load_lr():
            with nc.allow_non_contiguous_dma(reason="one rate for each partition and output tile"):
                nc.sync.dma_start(out=lr_sb[:, :, 0:1], in_=lr.rearrange("(n p o) -> p n o", p=P, o=1))

        def load_wd_scales():
            by_row = wd_scales.bitcast(I32).rearrange("a (q r) c -> r q a c", r=4)
            for r in range(4):
                nc.sync.dma_start(out=wd_sc[r:P:32, :, :], in_=by_row[r])

        tab = [sb([P, T], I32, "tab%d" % a) for a in range(2)]
        w1_raw = {(a, b): sb([P, PACK, COLS], F32, "w1_raw%d%d" % (a, b)) for a in range(2) for b in range(2)}
        w2_raw = {(0, 0): sb([P, PACK, N], F32, "w2_raw0")}
        for c0 in (0, MID):
            w2_raw[1, c0] = sb([P, PACK, MID], F32, "w2_raw1_%d" % c0)
        wd = [sb([P, N], I32, "wd%d" % a) for a in range(2)]

        def load_tab(a):
            nc.sync.dma_start(out=tab[a][:], in_=tab_words[a].rearrange("p c i -> p (c i)").bitcast(I32))

        def load_w1(a, b):
            part = w1[a * PASS : (a + 1) * PASS, b * COLS : (b + 1) * COLS]
            nc.sync.dma_start(out=w1_raw[a, b][:], in_=part.rearrange("(p j) c -> p j c", j=PACK))

        def load_w2(b, c0, c1):
            part = w2[b * PASS : (b + 1) * PASS, c0:c1]
            nc.sync.dma_start(out=w2_raw[b, c0][:], in_=part.rearrange("(p j) c -> p j c", j=PACK))

        def load_tab_scales():
            by_row = tab_scales.bitcast(I32).rearrange("a (q r) c -> r q a c", r=4)
            for r in range(4):
                nc.sync.dma_start(out=tab_sc[r:P:LOWER, :], in_=by_row[r])

        def load_wd(a):
            nc.sync.dma_start(out=wd[a][:], in_=wd_words[a].rearrange("p c i -> p (c i)").bitcast(I32))

        picked = sb([P, S // 4], I32, "picked")
        v_scales = [picked, moved]
        v_codes = {}

        def gather_scales():
            nc.vector.tensor_copy(picked[:].bitcast(U8), tab_sc[:].bitcast(U8).indirect(offsets[:]))

        def move_scales():
            nc.sync.dma_start(out=moved[0 : P - LOWER, :], in_=picked[LOWER:P, :])

        def gather_words(a, s):
            v_codes[a, s] = sb([P, COLS], U32, "v_codes%d%d" % (a, s))
            entries = offsets[:, s * (COLS // GROUP) : (s + 1) * (COLS // GROUP)]
            nc.vector.tensor_copy(v_codes[a, s][:], tab[a][:].bitcast(U32).indirect(entries))

        def table_operand(a, s, c0, width):
            return (v_codes[a, s][:, c0 : c0 + width].bitcast(E5M2),
                    v_scales[a][:].bitcast(U8)[:, s * COLS + c0 : s * COLS + c0 + width])

        def cast(engine, dst, src):
            if engine == "scalar":
                nc.scalar.copy(out=dst, in_=src)
            else:
                nc.vector.tensor_copy(out=dst, in_=src)

        rounded, codes, scales = {}, {}, {}

        def staged(key, width, on=None, at=0):
            if key not in rounded:
                rounded[key] = sb([P, PACK * width], BF16, "rounded_" + key, on, at)
            return rounded[key]

        def round_w1(engine, a, b, m0, m1):
            pairs = slice(m0 // 2, m1 // 2)
            dst = staged("w1_%d%d" % (a, b), COLS)[:].rearrange("p (t m e j) -> p m j e t", t=PACK, e=2, j=PACK)
            src = w1_raw[a, b][:].rearrange("p j (m e t) -> p m j e t", e=2, t=PACK)
            cast(engine, dst[:, pairs, :, :, :], src[:, pairs, :, :, :])

        def round_w2(engine, b, c0, c1, first=0):
            dst = staged("w2_%d" % b, COLS)[:, PACK * c0 : PACK * c1].rearrange("p (c e j) -> p c j e", e=2, j=PACK)
            src = w2_raw[b, first][:, :, c0 - first : c1 - first].rearrange("p j (c e) -> p c j e", e=2)
            cast(engine, dst, src)

        def round_w2_gpsimd(b, c0, c1, first=0, key=None):
            dst = rounded[key][:] if key else staged("w2_%d" % b, COLS)[:, PACK * c0 : PACK * c1]
            dst = dst.rearrange("p (c j) -> p c j", j=PACK)
            src = w2_raw[b, first][:, :, c0 - first : c1 - first].rearrange("p j c -> p c j")
            nc.gpsimd.tensor_scalar(out=dst, in0=src, scalar1=1.0, scalar2=0.0, op0=MULT, op1=ADD)

        def quantize(key, c0, c1, width, source=None, on=None, at=0):
            if key not in codes:
                codes[key] = sb([P, width], U32, "codes_" + key, on, at)
                scales[key] = sb([P, width], U8, "scales_" + key)
            values = rounded[key][:, PACK * c0 : PACK * c1] if source is None else rounded[source][:]
            nc.vector.quantize_mx(out=codes[key][:, c0:c1].bitcast(E4M3), scales=scales[key][:, c0:c1], in_=values)

        banks = {}

        def opened(bk):
            banks[bk] = psum.tile([P, COLS], F32, name="bank%d" % bk, tag="bank%d" % bk)
            return banks[bk]

        def hidden_pass(b, s, t, a):
            bk = (8 * b + 4 * s + t) % RING
            acc = opened(bk) if a == 0 else banks[bk]
            key = "w1_%d%d" % (a, b)
            cols = slice(t * P, (t + 1) * P)
            words, row_scales = table_operand(a, s, 0, COLS)
            nc.tensor.matmul_mx(out=acc[:], lhsT=codes[key][:, cols].bitcast(E4M3), lhsT_scale=scales[key][:, cols],
                                rhs=words, rhs_scale=row_scales, start=(a == 0), stop=(a == 1))

        tanh_out = {}

        def tanh_plane(b, s, t):
            if (b, s) not in tanh_out:
                tanh_out[b, s] = sb([P, PACK, COLS], F32, "tanh_out%d%d" % (b, s))
            nc.scalar.activation(out=tanh_out[b, s][:, t, :], in_=banks[(8 * b + 4 * s + t) % RING][:], func=TANH, bias=per_r[:, b, t : t + 1])

        def gain(b, s, c0, c1, key, on=None, at=0, from_psum=False):
            dst = staged(key, c1 - c0, on, at)[:].rearrange("p (c e t) -> p c t e", e=2, t=PACK)
            src = tanh_out[b, s][:, :, c0:c1].rearrange("p t (c e) -> p c t e", e=2)
            gains = turned[:, :, 2 + b] if from_psum else per_r[:, 2 + b, 0:PACK]
            gains = gains.unsqueeze(1).unsqueeze(3).to_broadcast([P, (c1 - c0) // 2, PACK, 2])
            nc.vector.tensor_tensor(out=dst, in0=src, in1=gains, op=MULT)

        def gain_by_planes(b, s, c0, c1, key, on=None, at=0):
            gained = sb([P, PACK, c1 - c0], BF16, "gained_" + key, on, at)
            for t in range(PACK):
                nc.scalar.activation(out=gained[:, t, :], in_=tanh_out[b, s][:, t, c0:c1], func=COPY,
                                     scale=per_r[:, 2 + b, t : t + 1])
            return gained

        def interleave(gained, key, width):
            dst = staged(key, width)[:].rearrange("p (c e t) -> p c t e", e=4, t=PACK)
            nc.vector.tensor_copy(out=dst, in_=gained[:].rearrange("p t (c e) -> p c t e", e=4))

        def sum_of(group, n):
            s, c0, width, bank_of = GROUPS[group]
            bk = bank_of[n]
            place = bank_of[:n].count(bk)
            return bk, slice(place * width, (place + 1) * width), place == 0, place == bank_of.count(bk) - 1

        def direct_passes(group, n, passes=(1, 0), opens=True):
            s, c0, width, bank_of = GROUPS[group]
            bk, where, first, last = sum_of(group, n)
            cols = slice(n * P, (n + 1) * P)
            for a in passes:
                start = first and opens and a == passes[0]
                acc = opened(bk) if start else banks[bk]
                words, row_scales = table_operand(a, s, c0, width)
                nc.tensor.matmul_mx(out=acc[:, where], lhsT=wd[a][:, cols].bitcast(E4M3),
                                    lhsT_scale=wd_sc[:, a, :].bitcast(U8)[:, cols],
                                    rhs=words, rhs_scale=row_scales, start=start, stop=False)

        def branch_pass(b, group, n, c0=0, c1=None):
            bk, where, first, last = sum_of(group, n)
            cols = slice(n * P, (n + 1) * P)
            wk, hk = "w2_%d" % b, "h_%d%s" % (b, group)
            width = GROUPS[group][2]
            c1 = width if c1 is None else c1
            nc.tensor.matmul_mx(out=banks[bk][:, where][:, c0:c1], lhsT=codes[wk][:, cols].bitcast(E4M3),
                                lhsT_scale=scales[wk][:, cols], rhs=codes[hk][:, c0:c1].bitcast(E4M3),
                                rhs_scale=scales[hk][:, c0:c1], start=False,
                                stop=(last and b == CLOSING[group] and c1 == width))

        out_tiles = out.rearrange("(n p) c -> p n c", p=P)

        def finish(engine, group, n0, count):
            s, c0, width, bank_of = GROUPS[group]
            res = sb([P, count, width], F32, "res_%s%d" % (group, n0))
            for i in range(count):
                bk, where, first, last = sum_of(group, n0 + i)
                acc = banks[bk][:, where]
                rate = lr_sb[:, n0 + i, 0:1]
                if engine == "scalar":
                    nc.scalar.activation(out=res[:, i, :], in_=acc, func=COPY, scale=rate)
                else:
                    nc.vector.tensor_scalar(out=res[:, i, :], in0=acc, scalar1=rate, scalar2=None, op0=MULT)
            first_col = s * COLS + c0
            nc.sync.dma_start(out=out_tiles[:, n0 : n0 + count, first_col : first_col + width], in_=res[:])

        load_vectors()
        load_w1(0, 0)
        load_tab_scales()
        load_tab(0)
        load_w1(1, 0)
        round_w1("scalar", 0, 0, 0, P)
        gather_scales()
        turn_vectors()
        load_tab(1)
        move_scales()
        load_w1(0, 1)
        load_w1(1, 1)
        load_w2(0, 0, N)
        load_wd_scales()
        load_wd(0)
        load_w2(1, 0, MID)
        load_wd(1)
        load_w2(1, MID, N)
        load_lr()
        quantize("w1_00", 0, COLS, COLS)
        gather_words(0, 0)
        gather_words(0, 1)
        round_w1("scalar", 1, 0, VECTOR_SHARE_10, P)
        round_w1("vector", 1, 0, 0, VECTOR_SHARE_10)
        quantize("w1_10", 0, COLS, COLS)
        gather_words(1, 0)
        gather_words(1, 1)
        round_w1("vector", 0, 1, 0, P)
        quantize("w1_01", 0, COLS, COLS)
        round_w1("vector", 1, 1, 0, P)
        quantize("w1_11", 0, MID, COLS)
        quantize("w1_11", MID, COLS, COLS)

        planes = [(b, s, t) for b in range(2) for s in range(2) for t in range(PACK)]
        for b, s, t in planes[:RING]:
            hidden_pass(b, s, t, 0)
        for u, (b, s, t) in enumerate(planes):
            hidden_pass(b, s, t, 1)
            tanh_plane(b, s, t)
            if u + RING < len(planes):
                hidden_pass(*planes[u + RING], 0)

        gain(0, 0, 0, EARLY, "h_0ha", on="w1_raw01")
        gain(0, 0, EARLY, COLS, "h_0hb", on="w1_raw11", from_psum=True)
        gained_0q = gain_by_planes(0, 1, 0, MID, "0q")
        staged("w2_0", COLS, on="rounded_w1_11")
        round_w2_gpsimd(0, 0, GPSIMD_SHARE)
        round_w2("vector", 0, GPSIMD_SHARE, COLS)
        quantize("h_0h", 0, EARLY, COLS, source="h_0ha")
        quantize("h_0h", EARLY, COLS, COLS, source="h_0hb")
        quantize("w2_0", 0, COLS, COLS)
        gain(1, 0, 0, COLS, "h_1h", on="w2_raw0", from_psum=True)
        staged("w2_1", COLS, on="rounded_w2_0")
        round_w2_gpsimd(1, 0, MID)
        round_w2("scalar", 1, 3 * P, COLS, MID)
        gained_1r = gain_by_planes(1, 1, MID, COLS, "1r")
        quantize("w2_1", 0, MID, COLS)
        quantize("h_1h", 0, COLS, COLS, on="w2_raw1_0")
        gain(1, 1, 0, MID, "h_1q", on="w2_raw1_0", at=2048, from_psum=True)
        staged("w2_1c", P, on="rounded_h_1h")
        round_w2_gpsimd(1, 2 * P, 3 * P, MID, key="w2_1c")
        quantize("w2_1", 3 * P, COLS, COLS)
        quantize("w2_1", 2 * P, 3 * P, COLS, source="w2_1c")
        staged("h_0q", MID, on="rounded_h_1h", at=2048)
        interleave(gained_0q, "h_0q", MID)
        quantize("h_1q", 0, MID, MID)
        quantize("h_0q", 0, MID, MID)
        staged("h_1r", MID, on="gained_0q")
        interleave(gained_1r, "h_1r", MID)
        gain(0, 1, MID, MID + P, "h_0r0", on="rounded_h_1q")
        quantize("h_1r", 0, MID, MID)
        gain(0, 1, MID + P, COLS, "h_0r128", on="rounded_h_1q", at=1024)
        for c0 in (0, P):
            quantize("h_0r", c0, c0 + P, MID, source="h_0r%d" % c0)

        for a in range(2):
            for n in range(OUT_TILES - 1):
                direct_passes("h", n, (a,), opens=(a == 0))
        direct_passes("h", OUT_TILES - 1)
        for n in range(OUT_TILES):
            branch_pass(0, "h", n)
        for n in range(OUT_TILES):
            direct_passes("q", n)
        for n0 in (0, 2):
            for n in range(n0, n0 + 2):
                branch_pass(1, "h", n)
                finish("scalar", "h", n, 1)
            for n in ((0, 1) if n0 == 0 else (2,)):
                direct_passes("r", n)
        for b in (1, 0):
            for n in range(OUT_TILES):
                branch_pass(b, "q", n)
        finish("scalar", "q", 0, 2)
        finish("scalar", "q", 2, 2)
        direct_passes("r", 3)
        for n in range(OUT_TILES):
            branch_pass(1, "r", n)
        for c0 in (0, P):
            for n in range(OUT_TILES):
                branch_pass(0, "r", n, c0, c0 + P)
        for n in range(OUT_TILES):
            finish("scalar" if n % 2 else "vector", "r", n, 1)
